import numpy as np
import ml_dtypes


def mxq(x, axis, fmt="e4m3"):
    dtype, down = {"e4m3": (ml_dtypes.float8_e4m3fn, 7), "e5m2": (ml_dtypes.float8_e5m2, 14)}[fmt]
    v = np.moveaxis(np.asarray(x, np.float32).astype(ml_dtypes.bfloat16).astype(np.float64), axis, -1)
    blocks = v.reshape(v.shape[:-1] + (-1, 32))
    amax = np.abs(blocks).max(-1, keepdims=True)
    byte = np.maximum(np.where(amax > 0, np.frexp(amax)[1] - 1 + 127, 0) - down, 1)
    scale = np.exp2(byte - 127.0)
    codes = (blocks / scale).astype(np.float32).astype(dtype).astype(np.float64)
    return np.moveaxis((codes * scale).reshape(v.shape), -1, axis)


WIDE = False


def mx_kscale(k):
    if not WIDE:
        return np.ones(k)
    levels = np.array([10, -10, 5, -5, 0])
    if k % 512:
        return np.exp2(np.random.permutation(np.resize(levels, k // 32))).repeat(32)
    a = np.empty((k // 512, 16))
    for p in range(k // 512):
        a[p, :8] = np.random.permutation(np.resize(levels, 8))
        for g in range(8):
            far = levels[np.abs(levels - a[p, g]) >= 10]
            a[p, g + 8] = far[np.random.randint(len(far))]
    return np.exp2(a.ravel()).repeat(32)


def f64(x):
    return np.asarray(x).astype(np.float64)


def striped(idx):
    return np.tile(idx.reshape(-1, 16).T, (8, 1)).astype(np.uint16)


def unstriped(offs):
    return offs[:16].T.reshape(-1).astype(np.int64)


def pack_weight(w):
    k, n = w.shape
    w = f64(np.asarray(w, np.float32).astype(ml_dtypes.bfloat16)).reshape(k // 32, 32, n)
    amax = np.abs(w).max(1)
    byte = np.clip(np.where(amax > 0, np.frexp(amax)[1] - 1 + 127 - 7, 1), 1, 254)
    scaled = (w * np.exp2(127.0 - byte)[:, None, :]).reshape(k, n).astype(np.float32)
    words = np.ascontiguousarray(scaled.reshape(k // 512, 128, 4, n).transpose(0, 1, 3, 2)).astype(ml_dtypes.float8_e4m3fn).view(np.uint8)
    return words, np.ascontiguousarray(byte.astype(np.uint8).reshape(k // 512, 16, n))


def unpack_weight(words, scales):
    g, p, n, _ = words.shape
    vals = np.ascontiguousarray(words).view(ml_dtypes.float8_e4m3fn).astype(np.float64) * np.repeat(np.exp2(scales.astype(np.float64) - 127.0), 8, axis=1)[..., None]
    return vals.transpose(0, 1, 3, 2).reshape(g * 512, n)


K, T, S, H, N = 512, 2048, 1024, 512, 256


def setup_inputs():
    n = np.random.standard_normal
    s = mx_kscale(K)[:, None]
    u = mx_kscale(H)
    packed_xT = pack_weight(n((K, T)) * s)
    return {
        "x_words": packed_xT[0],
        "x_scales": packed_xT[1],
        "w1": (n((K, H)) / np.sqrt(K) / s * u).astype(np.float32),
        "w2": (n((H, N)) / np.sqrt(H) / u[:, None]).astype(np.float32),
        "pos": (0.5 * n((H, S)) * u[:, None]).astype(np.float32),
        "offs": striped(np.random.permutation(T)[(T * np.random.uniform(0, 1, S) ** 4).astype(np.int64)]),
    }


def reference(x_words, x_scales, w1, w2, pos, offs):
    xq = unpack_weight(x_words, x_scales)[:, unstriped(offs)]
    h = (mxq(f64(w1), 0, "e4m3").T @ xq) + f64(pos)
    return mxq(f64(w2), 0, "e4m3").T @ mxq(h, 0, "e4m3")

@@ -1,0 +1,169 @@
+from contextlib import ExitStack
+
+import concourse.mybir as mybir
+
+K, T, S, H, N = 512, 2048, 1024, 512, 256
+FLOPS = 2 * K * H * S + 2 * H * N * S
+
+F32 = mybir.dt.float32
+BF16 = mybir.dt.bfloat16
+I32 = mybir.dt.int32
+U32 = mybir.dt.uint32
+U16 = mybir.dt.uint16
+U8 = mybir.dt.uint8
+FP8X4 = mybir.dt.float8_e4m3fn_x4
+ADD = mybir.AluOpType.add
+
+P = 128
+PACK = 4
+CHUNK = 128
+LOAD = 256
+W1_PIECES = ((0, 128), (128, 384), (384, 512))
+GROUPS = ((0, 256), (256, 512), (512, 768), (768, 896), (896, 1024))
+
+
+def tile_picked_embpos_none_p_kernel(tc, x_words, x_scales, w1, w2, pos, offs, out):
+    nc = tc.nc
+    with ExitStack() as ctx:
+        keep = ctx.enter_context(tc.tile_pool(name="keep", bufs=1))
+        hidden_banks = ctx.enter_context(tc.psum_pool(name="hidden_banks", bufs=5))
+        out_banks = ctx.enter_context(tc.psum_pool(name="out_banks", bufs=3))
+
+        offsets = keep.tile([P, S // 16], U16, name="offsets")
+        nc.sync.dma_start(offsets[:], offs)
+
+        w1_rows = w1.rearrange("(p j) c -> p j c", j=PACK)
+        w1_raw = [keep.tile([P, PACK, c1 - c0], F32, name=f"w1_raw{c0}", align_bytes=64) for c0, c1 in W1_PIECES]
+
+        def load_w1(i):
+            c0, c1 = W1_PIECES[i]
+            nc.sync.dma_start(out=w1_raw[i][:], in_=w1_rows[:, :, c0:c1])
+
+        table_scales = keep.tile([P, T], U8, name="table_scales", align_bytes=64)
+        nc.vector.memset(table_scales[:].bitcast(I32), 0)
+        load_w1(0)
+        for q in range(4):
+            nc.sync.dma_start(
+                out=table_scales[32 * q : 32 * q + 4, :].bitcast(I32),
+                in_=x_scales[0][4 * q : 4 * q + 4, :].bitcast(I32),
+            )
+        table_words = keep.tile([P, T], I32, name="table_words", align_bytes=64)
+        nc.sync.dma_start(out=table_words[:], in_=x_words[0].rearrange("p n t -> p (n t)").bitcast(I32))
+        load_w1(1)
+        load_w1(2)
+
+        pos_rows = pos.rearrange("(p t) n -> p t n", t=PACK)
+        pos_sb = []
+        w2_raw = keep.tile([P, PACK, N], F32, name="w2_raw", align_bytes=64)
+        for g in range(S // LOAD):
+            piece = keep.tile([P, PACK, LOAD], F32, name=f"pos{g}", align_bytes=64)
+            nc.sync.dma_start(out=piece[:], in_=pos_rows[:, :, g * LOAD : (g + 1) * LOAD])
+            pos_sb.append(piece)
+            if g == 1:
+                nc.sync.dma_start(out=w2_raw[:], in_=w2.rearrange("(p j) m -> p j m", j=PACK))
+
+        x_scale = keep.tile([P, S], U8, name="x_scale", align_bytes=64)
+        nc.vector.tensor_copy(x_scale[:], table_scales[:].indirect(offsets[:]))
+        x_codes = []
+        for g in range(S // LOAD):
+            codes = keep.tile([P, LOAD], U32, name=f"x_codes{g}", align_bytes=64)
+            x_codes.append(codes)
+
+        def gather_words(g):
+            cols = LOAD // 16
+            nc.vector.tensor_copy(
+                x_codes[g][:], table_words[:].bitcast(U32).indirect(offsets[:, g * cols : (g + 1) * cols])
+            )
+
+        gather_words(0)
+
+        w1_grouped = keep.tile([P, PACK, P, PACK], BF16, name="w1_grouped", align_bytes=64)
+        for (c0, c1), piece in zip(W1_PIECES, w1_raw):
+            nc.scalar.copy(
+                out=w1_grouped[:, :, c0 // PACK : c1 // PACK, :].rearrange("p t m j -> p m j t"),
+                in_=piece[:].rearrange("p j (m t) -> p m j t", t=PACK),
+            )
+        w1_codes = keep.tile([P, H], U32, name="w1_codes", align_bytes=64)
+        w1_scale = keep.tile([P, H], U8, name="w1_scale", align_bytes=64)
+        nc.vector.quantize_mx(
+            out=w1_codes[:].bitcast(FP8X4),
+            scales=w1_scale[:],
+            in_=w1_grouped[:].rearrange("p t m j -> p (t m j)"),
+        )
+
+        w2_grouped = keep.tile([P, N, PACK], BF16, name="w2_grouped", align_bytes=64)
+        w2_codes = keep.tile([P, N], U32, name="w2_codes", align_bytes=64)
+        w2_scale = keep.tile([P, N], U8, name="w2_scale", align_bytes=64)
+
+        def quantise_w2():
+            nc.scalar.copy(
+                out=w2_grouped[:].rearrange("p (c i) j -> p c j i", i=4),
+                in_=w2_raw[:].rearrange("p j (c i) -> p c j i", i=4),
+            )
+            nc.vector.quantize_mx(
+                out=w2_codes[:].bitcast(FP8X4),
+                scales=w2_scale[:],
+                in_=w2_grouped[:].rearrange("p m j -> p (m j)"),
+            )
+
+        hidden = [keep.tile([P, n1 - n0, PACK], BF16, name=f"hidden{n0}", align_bytes=64) for n0, n1 in GROUPS]
+
+        def first_layer(n0):
+            g, lo = divmod(n0, LOAD)
+            bank = hidden_banks.tile([P, PACK, CHUNK], F32, name="hidden_bank")
+            for t in range(PACK):
+                nc.tensor.matmul_mx(
+                    out=bank[:, t, :],
+                    lhsT=w1_codes[:, t * P : (t + 1) * P].bitcast(FP8X4),
+                    lhsT_scale=w1_scale[:, t * P : (t + 1) * P],
+                    rhs=x_codes[g][:, lo : lo + CHUNK].bitcast(FP8X4),
+                    rhs_scale=x_scale[:, n0 : n0 + CHUNK],
+                    start=True,
+                    stop=True,
+                )
+            k = [i for i, (a, b) in enumerate(GROUPS) if a <= n0 < b][0]
+            at = n0 - GROUPS[k][0]
+            nc.vector.tensor_tensor(
+                out=hidden[k][:, at : at + CHUNK, :].rearrange("p (c i) t -> p c t i", i=4),
+                in0=bank[:].rearrange("p t (c i) -> p c t i", i=4),
+                in1=pos_sb[g][:, :, lo : lo + CHUNK].rearrange("p t (c i) -> p c t i", i=4),
+                op=ADD,
+            )
+
+        out_rows = out.rearrange("(b p) n -> p b n", p=P)
+
+        def second_layer(k):
+            n0, n1 = GROUPS[k]
+            width = n1 - n0
+            codes = keep.tile([P, width], U32, name=f"h_codes{k}", align_bytes=64)
+            scale = keep.tile([P, width], U8, name=f"h_scale{k}", align_bytes=64)
+            nc.vector.quantize_mx(
+                out=codes[:].bitcast(FP8X4), scales=scale[:], in_=hidden[k][:].rearrange("p n t -> p (n t)")
+            )
+            bank = out_banks.tile([P, N // P, width], F32, name="out_bank")
+            for b in range(N // P):
+                nc.tensor.matmul_mx(
+                    out=bank[:, b, :],
+                    lhsT=w2_codes[:, b * P : (b + 1) * P].bitcast(FP8X4),
+                    lhsT_scale=w2_scale[:, b * P : (b + 1) * P],
+                    rhs=codes[:].bitcast(FP8X4),
+                    rhs_scale=scale[:],
+                    start=True,
+                    stop=True,
+                )
+            result = keep.tile([P, N // P, width], F32, name=f"result{k}", align_bytes=64)
+            nc.scalar.copy(out=result[:], in_=bank[:])
+            nc.sync.dma_start(out=out_rows[:, :, n0:n1], in_=result[:])
+
+        done = 0
+        for n0 in range(0, S, CHUNK):
+            if n0 % LOAD == 0 and n0 + LOAD < S:
+                gather_words(n0 // LOAD + 1)
+            first_layer(n0)
+            if n0 == CHUNK:
+                quantise_w2()
+            while GROUPS[done][1] <= n0:
+                second_layer(done)
+                done = done + 1
+        for k in range(done, len(GROUPS)):
+            second_layer(k)

@@ -18,16 +18,17 @@ P = 128
 PACK = 4
 CHUNK = 128
 LOAD = 256
-W1_PIECES = ((0, 128), (128, 384), (384, 512))
+W1_PIECES = ((0, 128), (128, 256), (256, 384), (384, 512))
 GROUPS = ((0, 256), (256, 512), (512, 768), (768, 896), (896, 1024))
+GATHERS = ((0, 768), (768, 1024))
 
 
 def tile_picked_embpos_none_p_kernel(tc, x_words, x_scales, w1, w2, pos, offs, out):
     nc = tc.nc
     with ExitStack() as ctx:
         keep = ctx.enter_context(tc.tile_pool(name="keep", bufs=1))
-        hidden_banks = ctx.enter_context(tc.psum_pool(name="hidden_banks", bufs=5))
-        out_banks = ctx.enter_context(tc.psum_pool(name="out_banks", bufs=3))
+        hidden_banks = ctx.enter_context(tc.psum_pool(name="hidden_banks", bufs=4))
+        out_banks = ctx.enter_context(tc.psum_pool(name="out_banks", bufs=4))
 
         offsets = keep.tile([P, S // 16], U16, name="offsets")
         nc.sync.dma_start(offsets[:], offs)
@@ -47,10 +48,11 @@ def tile_picked_embpos_none_p_kernel(tc, x_words, x_scales, w1, w2, pos, offs, o
                 out=table_scales[32 * q : 32 * q + 4, :].bitcast(I32),
                 in_=x_scales[0][4 * q : 4 * q + 4, :].bitcast(I32),
             )
+        load_w1(1)
         table_words = keep.tile([P, T], I32, name="table_words", align_bytes=64)
         nc.sync.dma_start(out=table_words[:], in_=x_words[0].rearrange("p n t -> p (n t)").bitcast(I32))
-        load_w1(1)
         load_w1(2)
+        load_w1(3)
 
         pos_rows = pos.rearrange("(p t) n -> p t n", t=PACK)
         pos_sb = []
@@ -65,19 +67,18 @@ def tile_picked_embpos_none_p_kernel(tc, x_words, x_scales, w1, w2, pos, offs, o
         x_scale = keep.tile([P, S], U8, name="x_scale", align_bytes=64)
         nc.vector.tensor_copy(x_scale[:], table_scales[:].indirect(offsets[:]))
         x_codes = []
-        for g in range(S // LOAD):
-            codes = keep.tile([P, LOAD], U32, name=f"x_codes{g}", align_bytes=64)
-            x_codes.append(codes)
 
         def gather_words(g):
-            cols = LOAD // 16
+            n0, n1 = GATHERS[g]
+            tag = "shared" if g == len(GATHERS) - 1 else f"x_codes{g}"
+            x_codes.append(keep.tile([P, n1 - n0], U32, name=f"x_codes{g}", tag=tag, align_bytes=64))
             nc.vector.tensor_copy(
-                x_codes[g][:], table_words[:].bitcast(U32).indirect(offsets[:, g * cols : (g + 1) * cols])
+                x_codes[g][:], table_words[:].bitcast(U32).indirect(offsets[:, n0 // 16 : n1 // 16])
             )
 
         gather_words(0)
 
-        w1_grouped = keep.tile([P, PACK, P, PACK], BF16, name="w1_grouped", align_bytes=64)
+        w1_grouped = keep.tile([P, PACK, P, PACK], BF16, name="w1_grouped", tag="shared", align_bytes=64)
         for (c0, c1), piece in zip(W1_PIECES, w1_raw):
             nc.scalar.copy(
                 out=w1_grouped[:, :, c0 // PACK : c1 // PACK, :].rearrange("p t m j -> p m j t"),
@@ -85,11 +86,14 @@ def tile_picked_embpos_none_p_kernel(tc, x_words, x_scales, w1, w2, pos, offs, o
             )
         w1_codes = keep.tile([P, H], U32, name="w1_codes", align_bytes=64)
         w1_scale = keep.tile([P, H], U8, name="w1_scale", align_bytes=64)
-        nc.vector.quantize_mx(
-            out=w1_codes[:].bitcast(FP8X4),
-            scales=w1_scale[:],
-            in_=w1_grouped[:].rearrange("p t m j -> p (t m j)"),
-        )
+        for t in range(0, PACK, 2):
+            nc.vector.quantize_mx(
+                out=w1_codes[:, t * P : (t + 2) * P].bitcast(FP8X4),
+                scales=w1_scale[:, t * P : (t + 2) * P],
+                in_=w1_grouped[:, t : t + 2, :, :].rearrange("p t m j -> p (t m j)"),
+            )
+
+        gather_words(1)
 
         w2_grouped = keep.tile([P, N, PACK], BF16, name="w2_grouped", align_bytes=64)
         w2_codes = keep.tile([P, N], U32, name="w2_codes", align_bytes=64)
@@ -97,8 +101,8 @@ def tile_picked_embpos_none_p_kernel(tc, x_words, x_scales, w1, w2, pos, offs, o
 
         def quantise_w2():
             nc.scalar.copy(
-                out=w2_grouped[:].rearrange("p (c i) j -> p c j i", i=4),
-                in_=w2_raw[:].rearrange("p j (c i) -> p c j i", i=4),
+                out=w2_grouped[:].rearrange("p (c i) j -> p c j i", i=2),
+                in_=w2_raw[:].rearrange("p j (c i) -> p c j i", i=2),
             )
             nc.vector.quantize_mx(
                 out=w2_codes[:].bitcast(FP8X4),
@@ -110,13 +114,15 @@ def tile_picked_embpos_none_p_kernel(tc, x_words, x_scales, w1, w2, pos, offs, o
 
         def first_layer(n0):
             g, lo = divmod(n0, LOAD)
+            xg = [i for i, (a, b) in enumerate(GATHERS) if a <= n0 < b][0]
+            xlo = n0 - GATHERS[xg][0]
             bank = hidden_banks.tile([P, PACK, CHUNK], F32, name="hidden_bank")
             for t in range(PACK):
                 nc.tensor.matmul_mx(
                     out=bank[:, t, :],
                     lhsT=w1_codes[:, t * P : (t + 1) * P].bitcast(FP8X4),
                     lhsT_scale=w1_scale[:, t * P : (t + 1) * P],
-                    rhs=x_codes[g][:, lo : lo + CHUNK].bitcast(FP8X4),
+                    rhs=x_codes[xg][:, xlo : xlo + CHUNK].bitcast(FP8X4),
                     rhs_scale=x_scale[:, n0 : n0 + CHUNK],
                     start=True,
                     stop=True,
@@ -124,9 +130,9 @@ def tile_picked_embpos_none_p_kernel(tc, x_words, x_scales, w1, w2, pos, offs, o
             k = [i for i, (a, b) in enumerate(GROUPS) if a <= n0 < b][0]
             at = n0 - GROUPS[k][0]
             nc.vector.tensor_tensor(
-                out=hidden[k][:, at : at + CHUNK, :].rearrange("p (c i) t -> p c t i", i=4),
-                in0=bank[:].rearrange("p t (c i) -> p c t i", i=4),
-                in1=pos_sb[g][:, :, lo : lo + CHUNK].rearrange("p t (c i) -> p c t i", i=4),
+                out=hidden[k][:, at : at + CHUNK, :].rearrange("p (c i) t -> p c t i", i=2),
+                in0=bank[:].rearrange("p t (c i) -> p c t i", i=2),
+                in1=pos_sb[g][:, :, lo : lo + CHUNK].rearrange("p t (c i) -> p c t i", i=2),
                 op=ADD,
             )
 
@@ -140,10 +146,11 @@ def tile_picked_embpos_none_p_kernel(tc, x_words, x_scales, w1, w2, pos, offs, o
             nc.vector.quantize_mx(
                 out=codes[:].bitcast(FP8X4), scales=scale[:], in_=hidden[k][:].rearrange("p n t -> p (n t)")
             )
-            bank = out_banks.tile([P, N // P, width], F32, name="out_bank")
+            last = k == len(GROUPS) - 1
+            halves = [out_banks.tile([P, width], F32, name="out_bank")[:] for b in range(N // P)]
             for b in range(N // P):
                 nc.tensor.matmul_mx(
-                    out=bank[:, b, :],
+                    out=halves[b],
                     lhsT=w2_codes[:, b * P : (b + 1) * P].bitcast(FP8X4),
                     lhsT_scale=w2_scale[:, b * P : (b + 1) * P],
                     rhs=codes[:].bitcast(FP8X4),
@@ -151,14 +158,20 @@ def tile_picked_embpos_none_p_kernel(tc, x_words, x_scales, w1, w2, pos, offs, o
                     start=True,
                     stop=True,
                 )
-            result = keep.tile([P, N // P, width], F32, name=f"result{k}", align_bytes=64)
-            nc.scalar.copy(out=result[:], in_=bank[:])
-            nc.sync.dma_start(out=out_rows[:, :, n0:n1], in_=result[:])
+            if last:
+                results = [keep.tile([P, width], F32, name=f"last_result{b}", align_bytes=64) for b in range(N // P)]
+                nc.scalar.copy(out=results[0][:], in_=halves[0])
+                nc.scalar.dma_start(out=out_rows[:, 0, n0:n1], in_=results[0][:])
+                nc.vector.tensor_copy(out=results[1][:], in_=halves[1])
+                nc.sync.dma_start(out=out_rows[:, 1, n0:n1], in_=results[1][:])
+            else:
+                result = keep.tile([P, N // P, width], F32, name=f"result{k}", align_bytes=64)
+                for b in range(N // P):
+                    nc.scalar.copy(out=result[:, b, :], in_=halves[b])
+                nc.sync.dma_start(out=out_rows[:, :, n0:n1], in_=result[:])
 
         done = 0
         for n0 in range(0, S, CHUNK):
-            if n0 % LOAD == 0 and n0 + LOAD < S:
-                gather_words(n0 // LOAD + 1)
             first_layer(n0)
             if n0 == CHUNK:
                 quantise_w2()

@@ -17,9 +17,11 @@ ADD = mybir.AluOpType.add
 P = 128
 PACK = 4
 CHUNK = 128
-LOAD = 256
+HALF = 64
 W1_PIECES = ((0, 128), (128, 256), (256, 384), (384, 512))
+POS_PIECES = ((0, 256), (256, 512), (512, 640), (640, 768), (768, 896), (896, 1024))
 GROUPS = ((0, 256), (256, 512), (512, 768), (768, 896), (896, 1024))
+FIRST_WORDS = 384
 GATHERS = ((0, 768), (768, 1024))
 
 
@@ -42,24 +44,24 @@ def tile_picked_embpos_none_p_kernel(tc, x_words, x_scales, w1, w2, pos, offs, o
 
         table_scales = keep.tile([P, T], U8, name="table_scales", align_bytes=64)
         nc.vector.memset(table_scales[:].bitcast(I32), 0)
-        load_w1(0)
-        for q in range(4):
-            nc.sync.dma_start(
-                out=table_scales[32 * q : 32 * q + 4, :].bitcast(I32),
-                in_=x_scales[0][4 * q : 4 * q + 4, :].bitcast(I32),
-            )
-        load_w1(1)
         table_words = keep.tile([P, T], I32, name="table_words", align_bytes=64)
-        nc.sync.dma_start(out=table_words[:], in_=x_words[0].rearrange("p n t -> p (n t)").bitcast(I32))
-        load_w1(2)
-        load_w1(3)
+        word_rows = x_words[0].rearrange("p n t -> p (n t)").bitcast(I32)
+        nc.sync.dma_start(out=table_words[:, :FIRST_WORDS], in_=word_rows[:, :FIRST_WORDS])
+        for r in range(4):
+            nc.sync.dma_start(
+                out=table_scales[r:P:32, :].bitcast(I32),
+                in_=x_scales[0][r:16:4, :].bitcast(I32),
+            )
+        nc.sync.dma_start(out=table_words[:, FIRST_WORDS:], in_=word_rows[:, FIRST_WORDS:])
+        for i in range(len(W1_PIECES)):
+            load_w1(i)
 
         pos_rows = pos.rearrange("(p t) n -> p t n", t=PACK)
         pos_sb = []
         w2_raw = keep.tile([P, PACK, N], F32, name="w2_raw", align_bytes=64)
-        for g in range(S // LOAD):
-            piece = keep.tile([P, PACK, LOAD], F32, name=f"pos{g}", align_bytes=64)
-            nc.sync.dma_start(out=piece[:], in_=pos_rows[:, :, g * LOAD : (g + 1) * LOAD])
+        for g, (n0, n1) in enumerate(POS_PIECES):
+            piece = keep.tile([P, PACK, n1 - n0], F32, name=f"pos{g}", align_bytes=64)
+            nc.sync.dma_start(out=piece[:], in_=pos_rows[:, :, n0:n1])
             pos_sb.append(piece)
             if g == 1:
                 nc.sync.dma_start(out=w2_raw[:], in_=w2.rearrange("(p j) m -> p j m", j=PACK))
@@ -78,20 +80,27 @@ def tile_picked_embpos_none_p_kernel(tc, x_words, x_scales, w1, w2, pos, offs, o
 
         gather_words(0)
 
-        w1_grouped = keep.tile([P, PACK, P, PACK], BF16, name="w1_grouped", tag="shared", align_bytes=64)
-        for (c0, c1), piece in zip(W1_PIECES, w1_raw):
-            nc.scalar.copy(
-                out=w1_grouped[:, :, c0 // PACK : c1 // PACK, :].rearrange("p t m j -> p m j t"),
-                in_=piece[:].rearrange("p j (m t) -> p m j t", t=PACK),
-            )
+        w1_grouped = [
+            keep.tile([P, PACK, HALF, PACK], BF16, name=f"w1_grouped{h}", tag=("w1_first", "shared")[h], align_bytes=64)
+            for h in range(2)
+        ]
         w1_codes = keep.tile([P, H], U32, name="w1_codes", align_bytes=64)
         w1_scale = keep.tile([P, H], U8, name="w1_scale", align_bytes=64)
-        for t in range(0, PACK, 2):
-            nc.vector.quantize_mx(
-                out=w1_codes[:, t * P : (t + 2) * P].bitcast(FP8X4),
-                scales=w1_scale[:, t * P : (t + 2) * P],
-                in_=w1_grouped[:, t : t + 2, :, :].rearrange("p t m j -> p (t m j)"),
+        for (c0, c1), piece in zip(W1_PIECES, w1_raw):
+            h, m0 = divmod(c0 // PACK, HALF)
+            m1 = m0 + (c1 - c0) // PACK
+            nc.scalar.copy(
+                out=w1_grouped[h][:, :, m0:m1, :].rearrange("p t m j -> p m j t"),
+                in_=piece[:].rearrange("p j (m t) -> p m j t", t=PACK),
             )
+            if m1 == HALF:
+                for t in range(PACK):
+                    cols = slice(t * P + h * HALF, t * P + (h + 1) * HALF)
+                    nc.vector.quantize_mx(
+                        out=w1_codes[:, cols].bitcast(FP8X4),
+                        scales=w1_scale[:, cols],
+                        in_=w1_grouped[h][:, t, :, :].rearrange("p m j -> p (m j)"),
+                    )
 
         gather_words(1)
 
@@ -113,7 +122,8 @@ def tile_picked_embpos_none_p_kernel(tc, x_words, x_scales, w1, w2, pos, offs, o
         hidden = [keep.tile([P, n1 - n0, PACK], BF16, name=f"hidden{n0}", align_bytes=64) for n0, n1 in GROUPS]
 
         def first_layer(n0):
-            g, lo = divmod(n0, LOAD)
+            g = [i for i, (a, b) in enumerate(POS_PIECES) if a <= n0 < b][0]
+            lo = n0 - POS_PIECES[g][0]
             xg = [i for i, (a, b) in enumerate(GATHERS) if a <= n0 < b][0]
             xlo = n0 - GATHERS[xg][0]
             bank = hidden_banks.tile([P, PACK, CHUNK], F32, name="hidden_bank")

@@ -16,31 +16,37 @@ ADD = mybir.AluOpType.add
 
 P = 128
 PACK = 4
+PER_COLUMN = 16
 CHUNK = 128
+HIDDEN_BANKS = 4
+OUT_BANKS = 4
 HALF = 64
-W1_PIECES = ((0, 128), (128, 256), (256, 384), (384, 512))
-POS_PIECES = ((0, 256), (256, 512), (512, 640), (640, 768), (768, 896), (896, 1024))
-GROUPS = ((0, 256), (256, 512), (512, 768), (768, 896), (896, 1024))
+
 FIRST_WORDS = 384
-GATHERS = ((0, 768), (768, 1024))
+W1_PIECE = 128
+GATHERS = ((0, 256), (512, 1024), (256, 512))
+POS_PIECES = ((0, 128), (128, 384), (384, 512), (512, 640), (640, 896), (896, 1024))
+W2_PIECE = 2
+GROUPS = ((0, 256), (256, 512), (512, 768), (768, 896), (896, 1024))
+SPLIT_GROUP = 2
+
+
+def piece_of(pieces, n0):
+    index = [i for i, (a, b) in enumerate(pieces) if a <= n0 < b][0]
+    return index, n0 - pieces[index][0]
 
 
 def tile_picked_embpos_none_p_kernel(tc, x_words, x_scales, w1, w2, pos, offs, out):
     nc = tc.nc
     with ExitStack() as ctx:
         keep = ctx.enter_context(tc.tile_pool(name="keep", bufs=1))
-        hidden_banks = ctx.enter_context(tc.psum_pool(name="hidden_banks", bufs=4))
-        out_banks = ctx.enter_context(tc.psum_pool(name="out_banks", bufs=4))
+        hidden_banks = ctx.enter_context(tc.psum_pool(name="hidden_banks", bufs=1))
+        out_banks = ctx.enter_context(tc.psum_pool(name="out_banks", bufs=OUT_BANKS))
 
-        offsets = keep.tile([P, S // 16], U16, name="offsets")
+        offsets = keep.tile([P, S // PER_COLUMN], U16, name="offsets")
         nc.sync.dma_start(offsets[:], offs)
 
-        w1_rows = w1.rearrange("(p j) c -> p j c", j=PACK)
-        w1_raw = [keep.tile([P, PACK, c1 - c0], F32, name=f"w1_raw{c0}", align_bytes=64) for c0, c1 in W1_PIECES]
-
-        def load_w1(i):
-            c0, c1 = W1_PIECES[i]
-            nc.sync.dma_start(out=w1_raw[i][:], in_=w1_rows[:, :, c0:c1])
+        w1_raw = [keep.tile([P, PACK, W1_PIECE], F32, name=f"w1_raw{i}", align_bytes=64) for i in range(H // W1_PIECE)]
 
         table_scales = keep.tile([P, T], U8, name="table_scales", align_bytes=64)
         nc.vector.memset(table_scales[:].bitcast(I32), 0)
@@ -53,59 +59,64 @@ def tile_picked_embpos_none_p_kernel(tc, x_words, x_scales, w1, w2, pos, offs, o
                 in_=x_scales[0][r:16:4, :].bitcast(I32),
             )
         nc.sync.dma_start(out=table_words[:, FIRST_WORDS:], in_=word_rows[:, FIRST_WORDS:])
-        for i in range(len(W1_PIECES)):
-            load_w1(i)
+
+        w1_rows = w1.rearrange("(p j) c -> p j c", j=PACK)
+        for i, raw in enumerate(w1_raw):
+            nc.sync.dma_start(out=raw[:], in_=w1_rows[:, :, i * W1_PIECE : (i + 1) * W1_PIECE])
 
         pos_rows = pos.rearrange("(p t) n -> p t n", t=PACK)
         pos_sb = []
         w2_raw = keep.tile([P, PACK, N], F32, name="w2_raw", align_bytes=64)
         for g, (n0, n1) in enumerate(POS_PIECES):
-            piece = keep.tile([P, PACK, n1 - n0], F32, name=f"pos{g}", align_bytes=64)
+            if g == W2_PIECE:
+                nc.sync.dma_start(out=w2_raw[:], in_=w2.rearrange("(p j) m -> p j m", j=PACK))
+            piece = keep.tile([P, PACK, n1 - n0], F32, name=f"pos{g}", tag=f"pos{g}", align_bytes=64)
             nc.sync.dma_start(out=piece[:], in_=pos_rows[:, :, n0:n1])
             pos_sb.append(piece)
-            if g == 1:
-                nc.sync.dma_start(out=w2_raw[:], in_=w2.rearrange("(p j) m -> p j m", j=PACK))
 
         x_scale = keep.tile([P, S], U8, name="x_scale", align_bytes=64)
         nc.vector.tensor_copy(x_scale[:], table_scales[:].indirect(offsets[:]))
         x_codes = []
 
-        def gather_words(g):
+        def gather_words(g, tag):
             n0, n1 = GATHERS[g]
-            tag = "shared" if g == len(GATHERS) - 1 else f"x_codes{g}"
             x_codes.append(keep.tile([P, n1 - n0], U32, name=f"x_codes{g}", tag=tag, align_bytes=64))
             nc.vector.tensor_copy(
-                x_codes[g][:], table_words[:].bitcast(U32).indirect(offsets[:, n0 // 16 : n1 // 16])
+                x_codes[g][:],
+                table_words[:].bitcast(U32).indirect(offsets[:, n0 // PER_COLUMN : n1 // PER_COLUMN]),
             )
 
-        gather_words(0)
+        gather_words(0, "x_codes0")
+        gather_words(1, "x_codes1")
 
         w1_grouped = [
-            keep.tile([P, PACK, HALF, PACK], BF16, name=f"w1_grouped{h}", tag=("w1_first", "shared")[h], align_bytes=64)
-            for h in range(2)
+            keep.tile([P, PACK, HALF, PACK], BF16, name=f"w1_grouped{half}", tag=f"w1_grouped{half}", align_bytes=64)
+            for half in range(2)
         ]
         w1_codes = keep.tile([P, H], U32, name="w1_codes", align_bytes=64)
         w1_scale = keep.tile([P, H], U8, name="w1_scale", align_bytes=64)
-        for (c0, c1), piece in zip(W1_PIECES, w1_raw):
-            h, m0 = divmod(c0 // PACK, HALF)
-            m1 = m0 + (c1 - c0) // PACK
-            nc.scalar.copy(
-                out=w1_grouped[h][:, :, m0:m1, :].rearrange("p t m j -> p m j t"),
-                in_=piece[:].rearrange("p j (m t) -> p m j t", t=PACK),
-            )
+        for i, raw in enumerate(w1_raw):
+            half, m0 = divmod(i * W1_PIECE // PACK, HALF)
+            m1 = m0 + W1_PIECE // PACK
+            t_step = 2 if i == len(w1_raw) - 1 else PACK
+            for t0 in range(0, PACK, t_step):
+                nc.scalar.copy(
+                    out=w1_grouped[half][:, t0 : t0 + t_step, m0:m1, :].rearrange("p t m j -> p m j t"),
+                    in_=raw[:].rearrange("p j (m t) -> p m j t", t=PACK)[:, :, :, t0 : t0 + t_step],
+                )
             if m1 == HALF:
                 for t in range(PACK):
-                    cols = slice(t * P + h * HALF, t * P + (h + 1) * HALF)
+                    cols = slice(t * P + half * HALF, t * P + (half + 1) * HALF)
                     nc.vector.quantize_mx(
                         out=w1_codes[:, cols].bitcast(FP8X4),
                         scales=w1_scale[:, cols],
-                        in_=w1_grouped[h][:, t, :, :].rearrange("p m j -> p (m j)"),
+                        in_=w1_grouped[half][:, t, :, :].rearrange("p m j -> p (m j)"),
                     )
 
-        gather_words(1)
+        gather_words(2, "w1_grouped1")
 
         w2_grouped = keep.tile([P, N, PACK], BF16, name="w2_grouped", align_bytes=64)
-        w2_codes = keep.tile([P, N], U32, name="w2_codes", align_bytes=64)
+        w2_codes = keep.tile([P, N], U32, name="w2_codes", tag=f"pos{W2_PIECE}", align_bytes=64)
         w2_scale = keep.tile([P, N], U8, name="w2_scale", align_bytes=64)
 
         def quantise_w2():
@@ -122,45 +133,54 @@ def tile_picked_embpos_none_p_kernel(tc, x_words, x_scales, w1, w2, pos, offs, o
         hidden = [keep.tile([P, n1 - n0, PACK], BF16, name=f"hidden{n0}", align_bytes=64) for n0, n1 in GROUPS]
 
         def first_layer(n0):
-            g = [i for i, (a, b) in enumerate(POS_PIECES) if a <= n0 < b][0]
-            lo = n0 - POS_PIECES[g][0]
-            xg = [i for i, (a, b) in enumerate(GATHERS) if a <= n0 < b][0]
-            xlo = n0 - GATHERS[xg][0]
-            bank = hidden_banks.tile([P, PACK, CHUNK], F32, name="hidden_bank")
+            g, in_pos = piece_of(POS_PIECES, n0)
+            gather, in_gather = piece_of(GATHERS, n0)
+            group, in_group = piece_of(GROUPS, n0)
+            bank = hidden_banks.tile(
+                [P, PACK, CHUNK], F32, name="hidden_bank", tag=f"bank{n0 // CHUNK % HIDDEN_BANKS}"
+            )
             for t in range(PACK):
                 nc.tensor.matmul_mx(
                     out=bank[:, t, :],
                     lhsT=w1_codes[:, t * P : (t + 1) * P].bitcast(FP8X4),
                     lhsT_scale=w1_scale[:, t * P : (t + 1) * P],
-                    rhs=x_codes[xg][:, xlo : xlo + CHUNK].bitcast(FP8X4),
+                    rhs=x_codes[gather][:, in_gather : in_gather + CHUNK].bitcast(FP8X4),
                     rhs_scale=x_scale[:, n0 : n0 + CHUNK],
                     start=True,
                     stop=True,
                 )
-            k = [i for i, (a, b) in enumerate(GROUPS) if a <= n0 < b][0]
-            at = n0 - GROUPS[k][0]
             nc.vector.tensor_tensor(
-                out=hidden[k][:, at : at + CHUNK, :].rearrange("p (c i) t -> p c t i", i=2),
+                out=hidden[group][:, in_group : in_group + CHUNK, :].rearrange("p (c i) t -> p c t i", i=2),
                 in0=bank[:].rearrange("p t (c i) -> p c t i", i=2),
-                in1=pos_sb[g][:, :, lo : lo + CHUNK].rearrange("p t (c i) -> p c t i", i=2),
+                in1=pos_sb[g][:, :, in_pos : in_pos + CHUNK].rearrange("p t (c i) -> p c t i", i=2),
                 op=ADD,
             )
 
+        h_packed = []
+
+        def quantise_hidden(group):
+            n0, n1 = GROUPS[group]
+            codes = keep.tile([P, n1 - n0], U32, name=f"h_codes{group}", align_bytes=64)
+            scale = keep.tile([P, n1 - n0], U8, name=f"h_scale{group}", align_bytes=64)
+            nc.vector.quantize_mx(
+                out=codes[:].bitcast(FP8X4), scales=scale[:], in_=hidden[group][:].rearrange("p n t -> p (n t)")
+            )
+            h_packed.append((codes, scale))
+
         out_rows = out.rearrange("(b p) n -> p b n", p=P)
 
-        def second_layer(k):
-            n0, n1 = GROUPS[k]
+        def second_layer(group):
+            n0, n1 = GROUPS[group]
             width = n1 - n0
-            codes = keep.tile([P, width], U32, name=f"h_codes{k}", align_bytes=64)
-            scale = keep.tile([P, width], U8, name=f"h_scale{k}", align_bytes=64)
-            nc.vector.quantize_mx(
-                out=codes[:].bitcast(FP8X4), scales=scale[:], in_=hidden[k][:].rearrange("p n t -> p (n t)")
-            )
-            last = k == len(GROUPS) - 1
-            halves = [out_banks.tile([P, width], F32, name="out_bank")[:] for b in range(N // P)]
+            codes, scale = h_packed[group]
+            last = group == len(GROUPS) - 1
+            if last:
+                products = [hidden_banks.tile([P, width], F32, name="last_bank", tag=f"bank{b}") for b in range(N // P)]
+            else:
+                products = [out_banks.tile([P, width], F32, name="out_bank") for b in range(N // P)]
             for b in range(N // P):
                 nc.tensor.matmul_mx(
-                    out=halves[b],
+                    out=products[b][:],
                     lhsT=w2_codes[:, b * P : (b + 1) * P].bitcast(FP8X4),
                     lhsT_scale=w2_scale[:, b * P : (b + 1) * P],
                     rhs=codes[:].bitcast(FP8X4),
@@ -168,25 +188,31 @@ def tile_picked_embpos_none_p_kernel(tc, x_words, x_scales, w1, w2, pos, offs, o
                     start=True,
                     stop=True,
                 )
-            if last:
-                results = [keep.tile([P, width], F32, name=f"last_result{b}", align_bytes=64) for b in range(N // P)]
-                nc.scalar.copy(out=results[0][:], in_=halves[0])
-                nc.scalar.dma_start(out=out_rows[:, 0, n0:n1], in_=results[0][:])
-                nc.vector.tensor_copy(out=results[1][:], in_=halves[1])
-                nc.sync.dma_start(out=out_rows[:, 1, n0:n1], in_=results[1][:])
-            else:
-                result = keep.tile([P, N // P, width], F32, name=f"result{k}", align_bytes=64)
+            if group == SPLIT_GROUP:
                 for b in range(N // P):
-                    nc.scalar.copy(out=result[:, b, :], in_=halves[b])
+                    part = keep.tile([P, width], F32, name=f"result_part{b}", align_bytes=64)
+                    nc.scalar.copy(out=part[:], in_=products[b][:])
+                    nc.sync.dma_start(out=out_rows[:, b, n0:n1], in_=part[:])
+            else:
+                result = keep.tile([P, N // P, width], F32, name=f"result{group}", align_bytes=64)
+                nc.scalar.copy(out=result[:, 0, :], in_=products[0][:])
+                if last:
+                    nc.vector.tensor_copy(out=result[:, 1, :], in_=products[1][:])
+                else:
+                    nc.scalar.copy(out=result[:, 1, :], in_=products[1][:])
                 nc.sync.dma_start(out=out_rows[:, :, n0:n1], in_=result[:])
 
-        done = 0
+        w2_chunk = POS_PIECES[W2_PIECE][0]
+        multiplied = 0
         for n0 in range(0, S, CHUNK):
             first_layer(n0)
-            if n0 == CHUNK:
+            while GROUPS[len(h_packed)][1] <= n0:
+                quantise_hidden(len(h_packed))
+            if n0 == w2_chunk:
                 quantise_w2()
-            while GROUPS[done][1] <= n0:
-                second_layer(done)
-                done = done + 1
-        for k in range(done, len(GROUPS)):
-            second_layer(k)
+            while n0 >= w2_chunk and multiplied < len(h_packed):
+                second_layer(multiplied)
+                multiplied = multiplied + 1
+        for group in range(multiplied, len(GROUPS)):
+            quantise_hidden(group)
+            second_layer(group)

@@ -22,9 +22,9 @@ HIDDEN_BANKS = 4
 OUT_BANKS = 4
 HALF = 64
 
-FIRST_WORDS = 384
+FIRST_WORDS = 768
 W1_PIECE = 128
-GATHERS = ((0, 256), (512, 1024), (256, 512))
+GATHERS = ((0, 512), (512, 1024))
 POS_PIECES = ((0, 128), (128, 384), (384, 512), (512, 640), (640, 896), (896, 1024))
 W2_PIECE = 2
 GROUPS = ((0, 256), (256, 512), (512, 768), (768, 896), (896, 1024))
@@ -46,7 +46,7 @@ def tile_picked_embpos_none_p_kernel(tc, x_words, x_scales, w1, w2, pos, offs, o
         offsets = keep.tile([P, S // PER_COLUMN], U16, name="offsets")
         nc.sync.dma_start(offsets[:], offs)
 
-        w1_raw = [keep.tile([P, PACK, W1_PIECE], F32, name=f"w1_raw{i}", align_bytes=64) for i in range(H // W1_PIECE)]
+        w1_raw = [keep.tile([P, PACK, W1_PIECE], F32, name=f"w1_raw{i}", tag=f"w1_raw{i}", align_bytes=64) for i in range(H // W1_PIECE)]
 
         table_scales = keep.tile([P, T], U8, name="table_scales", align_bytes=64)
         nc.vector.memset(table_scales[:].bitcast(I32), 0)
@@ -54,7 +54,8 @@ def tile_picked_embpos_none_p_kernel(tc, x_words, x_scales, w1, w2, pos, offs, o
         word_rows = x_words[0].rearrange("p n t -> p (n t)").bitcast(I32)
         nc.sync.dma_start(out=table_words[:, :FIRST_WORDS], in_=word_rows[:, :FIRST_WORDS])
         for r in range(4):
-            nc.sync.dma_start(
+            queue = nc.sync if r % 2 == 0 else nc.scalar
+            queue.dma_start(
                 out=table_scales[r:P:32, :].bitcast(I32),
                 in_=x_scales[0][r:16:4, :].bitcast(I32),
             )
@@ -87,7 +88,6 @@ def tile_picked_embpos_none_p_kernel(tc, x_words, x_scales, w1, w2, pos, offs, o
             )
 
         gather_words(0, "x_codes0")
-        gather_words(1, "x_codes1")
 
         w1_grouped = [
             keep.tile([P, PACK, HALF, PACK], BF16, name=f"w1_grouped{half}", tag=f"w1_grouped{half}", align_bytes=64)
@@ -100,7 +100,8 @@ def tile_picked_embpos_none_p_kernel(tc, x_words, x_scales, w1, w2, pos, offs, o
             m1 = m0 + W1_PIECE // PACK
             t_step = 2 if i == len(w1_raw) - 1 else PACK
             for t0 in range(0, PACK, t_step):
-                nc.scalar.copy(
+                copy = nc.vector.tensor_copy if t0 == 2 else nc.scalar.copy
+                copy(
                     out=w1_grouped[half][:, t0 : t0 + t_step, m0:m1, :].rearrange("p t m j -> p m j t"),
                     in_=raw[:].rearrange("p j (m t) -> p m j t", t=PACK)[:, :, :, t0 : t0 + t_step],
                 )
@@ -113,7 +114,7 @@ def tile_picked_embpos_none_p_kernel(tc, x_words, x_scales, w1, w2, pos, offs, o
                         in_=w1_grouped[half][:, t, :, :].rearrange("p m j -> p (m j)"),
                     )
 
-        gather_words(2, "w1_grouped1")
+        gather_words(1, "w1_raw3")
 
         w2_grouped = keep.tile([P, N, PACK], BF16, name="w2_grouped", align_bytes=64)
         w2_codes = keep.tile([P, N], U32, name="w2_codes", tag=f"pos{W2_PIECE}", align_bytes=64)
@@ -196,7 +197,7 @@ def tile_picked_embpos_none_p_kernel(tc, x_words, x_scales, w1, w2, pos, offs, o
             else:
                 result = keep.tile([P, N // P, width], F32, name=f"result{group}", align_bytes=64)
                 nc.scalar.copy(out=result[:, 0, :], in_=products[0][:])
-                if last:
+                if group > SPLIT_GROUP:
                     nc.vector.tensor_copy(out=result[:, 1, :], in_=products[1][:])
                 else:
                     nc.scalar.copy(out=result[:, 1, :], in_=products[1][:])

@@ -25,8 +25,9 @@ HALF = 64
 FIRST_WORDS = 768
 W1_PIECE = 128
 GATHERS = ((0, 512), (512, 1024))
-POS_PIECES = ((0, 128), (128, 384), (384, 512), (512, 640), (640, 896), (896, 1024))
-W2_PIECE = 2
+POS_PIECES = ((0, 256), (256, 384), (384, 640), (640, 768), (768, 896), (896, 1024))
+W2_PIECE = 1
+GP = 96
 GROUPS = ((0, 256), (256, 512), (512, 768), (768, 896), (896, 1024))
 SPLIT_GROUP = 2
 
@@ -40,6 +41,7 @@ def tile_picked_embpos_none_p_kernel(tc, x_words, x_scales, w1, w2, pos, offs, o
     nc = tc.nc
     with ExitStack() as ctx:
         keep = ctx.enter_context(tc.tile_pool(name="keep", bufs=1))
+        shared = ctx.enter_context(tc.tile_pool(name="shared", bufs=1))
         hidden_banks = ctx.enter_context(tc.psum_pool(name="hidden_banks", bufs=1))
         out_banks = ctx.enter_context(tc.psum_pool(name="out_banks", bufs=OUT_BANKS))
 
@@ -116,104 +118,150 @@ def tile_picked_embpos_none_p_kernel(tc, x_words, x_scales, w1, w2, pos, offs, o
 
         gather_words(1, "w1_raw3")
 
-        w2_grouped = keep.tile([P, N, PACK], BF16, name="w2_grouped", align_bytes=64)
-        w2_codes = keep.tile([P, N], U32, name="w2_codes", tag=f"pos{W2_PIECE}", align_bytes=64)
+        w2_grouped = keep.tile([P, N, PACK], BF16, name="w2_grouped", tag="w2_grouped", align_bytes=64)
+        w2_codes = keep.tile([P, N], U32, name="w2_codes", tag="pos1", align_bytes=64)
         w2_scale = keep.tile([P, N], U8, name="w2_scale", align_bytes=64)
+        nc.scalar.copy(
+            out=w2_grouped[:].rearrange("p (c i) j -> p c j i", i=2),
+            in_=w2_raw[:].rearrange("p j (c i) -> p c j i", i=2),
+        )
 
         def quantise_w2():
-            nc.scalar.copy(
-                out=w2_grouped[:].rearrange("p (c i) j -> p c j i", i=2),
-                in_=w2_raw[:].rearrange("p j (c i) -> p c j i", i=2),
-            )
             nc.vector.quantize_mx(
                 out=w2_codes[:].bitcast(FP8X4),
                 scales=w2_scale[:],
                 in_=w2_grouped[:].rearrange("p m j -> p (m j)"),
             )
 
-        hidden = [keep.tile([P, n1 - n0, PACK], BF16, name=f"hidden{n0}", align_bytes=64) for n0, n1 in GROUPS]
+        banks_used = []
 
-        def first_layer(n0):
-            g, in_pos = piece_of(POS_PIECES, n0)
+        def first_product(n0, width):
             gather, in_gather = piece_of(GATHERS, n0)
-            group, in_group = piece_of(GROUPS, n0)
-            bank = hidden_banks.tile(
-                [P, PACK, CHUNK], F32, name="hidden_bank", tag=f"bank{n0 // CHUNK % HIDDEN_BANKS}"
-            )
+            bank = hidden_banks.tile([P, PACK, width], F32, name="hidden_bank", tag=f"bank{len(banks_used) % HIDDEN_BANKS}")
+            banks_used.append(bank)
             for t in range(PACK):
                 nc.tensor.matmul_mx(
                     out=bank[:, t, :],
                     lhsT=w1_codes[:, t * P : (t + 1) * P].bitcast(FP8X4),
                     lhsT_scale=w1_scale[:, t * P : (t + 1) * P],
-                    rhs=x_codes[gather][:, in_gather : in_gather + CHUNK].bitcast(FP8X4),
-                    rhs_scale=x_scale[:, n0 : n0 + CHUNK],
+                    rhs=x_codes[gather][:, in_gather : in_gather + width].bitcast(FP8X4),
+                    rhs_scale=x_scale[:, n0 : n0 + width],
                     start=True,
                     stop=True,
                 )
+            return bank
+
+        def add_pos(n0, width, target):
+            g, in_pos = piece_of(POS_PIECES, n0)
+            bank = first_product(n0, width)
             nc.vector.tensor_tensor(
-                out=hidden[group][:, in_group : in_group + CHUNK, :].rearrange("p (c i) t -> p c t i", i=2),
+                out=target.rearrange("p (c i) t -> p c t i", i=2),
                 in0=bank[:].rearrange("p t (c i) -> p c t i", i=2),
-                in1=pos_sb[g][:, :, in_pos : in_pos + CHUNK].rearrange("p t (c i) -> p c t i", i=2),
+                in1=pos_sb[g][:, :, in_pos : in_pos + width].rearrange("p t (c i) -> p c t i", i=2),
                 op=ADD,
             )
 
-        h_packed = []
+        def quantise(codes, scale, values):
+            nc.vector.quantize_mx(out=codes.bitcast(FP8X4), scales=scale, in_=values.rearrange("p n t -> p (n t)"))
 
-        def quantise_hidden(group):
-            n0, n1 = GROUPS[group]
-            codes = keep.tile([P, n1 - n0], U32, name=f"h_codes{group}", align_bytes=64)
-            scale = keep.tile([P, n1 - n0], U8, name=f"h_scale{group}", align_bytes=64)
-            nc.vector.quantize_mx(
-                out=codes[:].bitcast(FP8X4), scales=scale[:], in_=hidden[group][:].rearrange("p n t -> p (n t)")
+        def second_product(product, b, codes, scale):
+            nc.tensor.matmul_mx(
+                out=product,
+                lhsT=w2_codes[:, b * P : (b + 1) * P].bitcast(FP8X4),
+                lhsT_scale=w2_scale[:, b * P : (b + 1) * P],
+                rhs=codes.bitcast(FP8X4),
+                rhs_scale=scale,
+                start=True,
+                stop=True,
             )
-            h_packed.append((codes, scale))
 
         out_rows = out.rearrange("(b p) n -> p b n", p=P)
 
-        def second_layer(group):
-            n0, n1 = GROUPS[group]
-            width = n1 - n0
-            codes, scale = h_packed[group]
-            last = group == len(GROUPS) - 1
-            if last:
-                products = [hidden_banks.tile([P, width], F32, name="last_bank", tag=f"bank{b}") for b in range(N // P)]
-            else:
-                products = [out_banks.tile([P, width], F32, name="out_bank") for b in range(N // P)]
-            for b in range(N // P):
-                nc.tensor.matmul_mx(
-                    out=products[b][:],
-                    lhsT=w2_codes[:, b * P : (b + 1) * P].bitcast(FP8X4),
-                    lhsT_scale=w2_scale[:, b * P : (b + 1) * P],
-                    rhs=codes[:].bitcast(FP8X4),
-                    rhs_scale=scale[:],
-                    start=True,
-                    stop=True,
-                )
-            if group == SPLIT_GROUP:
-                for b in range(N // P):
-                    part = keep.tile([P, width], F32, name=f"result_part{b}", align_bytes=64)
-                    nc.scalar.copy(out=part[:], in_=products[b][:])
-                    nc.sync.dma_start(out=out_rows[:, b, n0:n1], in_=part[:])
-            else:
-                result = keep.tile([P, N // P, width], F32, name=f"result{group}", align_bytes=64)
-                nc.scalar.copy(out=result[:, 0, :], in_=products[0][:])
-                if group > SPLIT_GROUP:
-                    nc.vector.tensor_copy(out=result[:, 1, :], in_=products[1][:])
-                else:
-                    nc.scalar.copy(out=result[:, 1, :], in_=products[1][:])
-                nc.sync.dma_start(out=out_rows[:, :, n0:n1], in_=result[:])
+        def second_layer(codes, scale, width, targets, copies):
+            for b in range(2):
+                product = out_banks.tile([P, width], F32, name="out_bank")
+                second_product(product[:], b, codes, scale)
+                copies[b](out=targets[b], in_=product[:])
 
-        w2_chunk = POS_PIECES[W2_PIECE][0]
-        multiplied = 0
-        for n0 in range(0, S, CHUNK):
-            first_layer(n0)
-            while GROUPS[len(h_packed)][1] <= n0:
-                quantise_hidden(len(h_packed))
-            if n0 == w2_chunk:
-                quantise_w2()
-            while n0 >= w2_chunk and multiplied < len(h_packed):
-                second_layer(multiplied)
-                multiplied = multiplied + 1
-        for group in range(multiplied, len(GROUPS)):
-            quantise_hidden(group)
-            second_layer(group)
+        def sbuf(shape, dtype, name, tag=None):
+            return keep.tile(shape, dtype, name=name, tag=tag or name, align_bytes=64)
+
+        scalar_only = (nc.scalar.copy, nc.scalar.copy)
+        both = (nc.scalar.copy, nc.vector.tensor_copy)
+        h_scale = sbuf([P, S], U8, "h_scale")
+
+        hidden0 = sbuf([P, 256, PACK], BF16, "hidden0")
+        hidden1 = sbuf([P, 128, PACK], BF16, "hidden1")
+        add_pos(0, 128, hidden0[:, :128, :])
+        add_pos(128, 128, hidden0[:, 128:, :])
+        add_pos(256, 128, hidden1[:])
+        bank = first_product(384, 128)
+        shared_bank = bank
+        product = shared.tile([P, GP, PACK], F32, name="product", offset=0, align_bytes=64)
+        nc.scalar.copy(out=product[:], in_=bank[:, :, :GP].rearrange("p t n -> p n t"))
+        codes0 = sbuf([P, 384], U32, "codes0")
+        quantise(codes0[:, :256], h_scale[:, 0:256], hidden0[:])
+        quantise(codes0[:, 256:], h_scale[:, 256:384], hidden1[:])
+        quantise_w2()
+        hidden2 = sbuf([P, 128, PACK], BF16, "hidden2", "w2_grouped")
+        nc.gpsimd.tensor_tensor(
+            out=hidden2[:, :GP, :], in0=product[:], in1=pos_sb[2][:, :, :GP].rearrange("p t n -> p n t"), op=ADD
+        )
+        result0 = sbuf([P, 2, 384], F32, "result0")
+        second_layer(codes0[:, :256], h_scale[:, 0:256], 256, [result0[:, b, :256] for b in range(2)], scalar_only)
+        second_layer(codes0[:, 256:], h_scale[:, 256:384], 128, [result0[:, b, 256:] for b in range(2)], scalar_only)
+        nc.sync.dma_start(out=out_rows[:, :, 0:384], in_=result0[:])
+
+        hidden3 = sbuf([P, 256, PACK], BF16, "hidden3")
+        hidden4 = sbuf([P, 128, PACK], BF16, "hidden4")
+        add_pos(512, 128, hidden3[:, :128, :])
+        nc.vector.tensor_tensor(
+            out=hidden2[:, GP:, :].rearrange("p (c i) t -> p c t i", i=2),
+            in0=shared_bank[:, :, GP:].rearrange("p t (c i) -> p c t i", i=2),
+            in1=pos_sb[2][:, :, GP:128].rearrange("p t (c i) -> p c t i", i=2),
+            op=ADD,
+        )
+        add_pos(640, 128, hidden3[:, 128:, :])
+        add_pos(768, 128, hidden4[:])
+
+        codes2 = sbuf([P, 128], U32, "codes2")
+        quantise(codes2[:], h_scale[:, 384:512], hidden2[:])
+        result2 = sbuf([P, 2, 128], F32, "result2")
+        second_layer(codes2[:], h_scale[:, 384:512], 128, [result2[:, b, :] for b in range(2)], scalar_only)
+        nc.sync.dma_start(out=out_rows[:, :, 384:512], in_=result2[:])
+
+        codes3 = shared.tile([P, 256], U32, name="codes3", offset=0, align_bytes=64)
+        quantise(codes3[:], h_scale[:, 512:768], hidden3[:])
+        for b in range(2):
+            bank = out_banks.tile([P, 256], F32, name="out_bank")
+            second_product(bank[:], b, codes3[:], h_scale[:, 512:768])
+            part = sbuf([P, 256], F32, f"part{b}")
+            nc.scalar.copy(out=part[:], in_=bank[:])
+            nc.sync.dma_start(out=out_rows[:, b, 512:768], in_=part[:])
+
+        hidden5 = shared.tile([P, 64, PACK], BF16, name="hidden5", offset=1024, align_bytes=64)
+        add_pos(896, 64, hidden5[:])
+        codes4 = sbuf([P, 128], U32, "codes4", "pos2")
+        quantise(codes4[:], h_scale[:, 768:896], hidden4[:])
+        hidden6 = sbuf([P, 64, PACK], BF16, "hidden6", "hidden3")
+        add_pos(960, 64, hidden6[:])
+        codes5 = sbuf([P, 128], U32, "codes5", "product_late")
+        quantise(codes5[:, :64], h_scale[:, 896:960], hidden5[:])
+        quantise(codes5[:, 64:], h_scale[:, 960:1024], hidden6[:])
+
+        result4 = sbuf([P, 2, 128], F32, "result4")
+        banks4 = [hidden_banks.tile([P, 128], F32, name="late_bank", tag=f"bank{b + 1}") for b in range(2)]
+        for b in range(2):
+            second_product(banks4[b][:], b, codes4[:], h_scale[:, 768:896])
+        for b in range(2):
+            scalar_only[b](out=result4[:, b, :], in_=banks4[b][:])
+        nc.sync.dma_start(out=out_rows[:, :, 768:896], in_=result4[:])
+
+        result5 = sbuf([P, 2, 128], F32, "result5")
+        banks5 = [out_banks.tile([P, 128], F32, name="out_bank") for b in range(2)]
+        for c in (0, 64):
+            for b in range(2):
+                second_product(banks5[b][:, c : c + 64], b, codes5[:, c : c + 64], h_scale[:, 896 + c : 960 + c])
+        for b in range(2):
+            both[b](out=result5[:, b, :], in_=banks5[b][:])
+        nc.sync.dma_start(out=out_rows[:, :, 896:1024], in_=result5[:])

@@ -20,16 +20,17 @@ PER_COLUMN = 16
 CHUNK = 128
 HIDDEN_BANKS = 4
 OUT_BANKS = 4
+OUT_TILES = N // P
 HALF = 64
 
 FIRST_WORDS = 768
 W1_PIECE = 128
 GATHERS = ((0, 512), (512, 1024))
-POS_PIECES = ((0, 256), (256, 384), (384, 640), (640, 768), (768, 896), (896, 1024))
+GPSIMD_ENTRIES = 96
+POS_PIECES = ((0, 256), (256, 416), (416, 640), (640, 768), (768, 896), (896, 1024))
 W2_PIECE = 1
-GP = 96
-GROUPS = ((0, 256), (256, 512), (512, 768), (768, 896), (896, 1024))
-SPLIT_GROUP = 2
+GPSIMD_PIECE = 2
+LAST_HALF = CHUNK // 2
 
 
 def piece_of(pieces, n0):
@@ -41,18 +42,21 @@ def tile_picked_embpos_none_p_kernel(tc, x_words, x_scales, w1, w2, pos, offs, o
     nc = tc.nc
     with ExitStack() as ctx:
         keep = ctx.enter_context(tc.tile_pool(name="keep", bufs=1))
-        shared = ctx.enter_context(tc.tile_pool(name="shared", bufs=1))
+        behind_gpsimd = ctx.enter_context(tc.tile_pool(name="behind_gpsimd", bufs=1))
         hidden_banks = ctx.enter_context(tc.psum_pool(name="hidden_banks", bufs=1))
         out_banks = ctx.enter_context(tc.psum_pool(name="out_banks", bufs=OUT_BANKS))
+
+        def sbuf(shape, dtype, name, takes_over=None):
+            return keep.tile(shape, dtype, name=name, tag=takes_over or name, align_bytes=64)
 
         offsets = keep.tile([P, S // PER_COLUMN], U16, name="offsets")
         nc.sync.dma_start(offsets[:], offs)
 
-        w1_raw = [keep.tile([P, PACK, W1_PIECE], F32, name=f"w1_raw{i}", tag=f"w1_raw{i}", align_bytes=64) for i in range(H // W1_PIECE)]
+        w1_raw = [sbuf([P, PACK, W1_PIECE], F32, f"w1_raw{i}") for i in range(H // W1_PIECE)]
 
-        table_scales = keep.tile([P, T], U8, name="table_scales", align_bytes=64)
+        table_scales = sbuf([P, T], U8, "table_scales")
         nc.vector.memset(table_scales[:].bitcast(I32), 0)
-        table_words = keep.tile([P, T], I32, name="table_words", align_bytes=64)
+        table_words = sbuf([P, T], I32, "table_words")
         word_rows = x_words[0].rearrange("p n t -> p (n t)").bitcast(I32)
         nc.sync.dma_start(out=table_words[:, :FIRST_WORDS], in_=word_rows[:, :FIRST_WORDS])
         for r in range(4):
@@ -69,76 +73,78 @@ def tile_picked_embpos_none_p_kernel(tc, x_words, x_scales, w1, w2, pos, offs, o
 
         pos_rows = pos.rearrange("(p t) n -> p t n", t=PACK)
         pos_sb = []
-        w2_raw = keep.tile([P, PACK, N], F32, name="w2_raw", align_bytes=64)
+        w2_raw = sbuf([P, PACK, N], F32, "w2_raw")
         for g, (n0, n1) in enumerate(POS_PIECES):
             if g == W2_PIECE:
                 nc.sync.dma_start(out=w2_raw[:], in_=w2.rearrange("(p j) m -> p j m", j=PACK))
-            piece = keep.tile([P, PACK, n1 - n0], F32, name=f"pos{g}", tag=f"pos{g}", align_bytes=64)
+            piece = sbuf([P, PACK, n1 - n0], F32, f"pos{g}")
             nc.sync.dma_start(out=piece[:], in_=pos_rows[:, :, n0:n1])
             pos_sb.append(piece)
 
-        x_scale = keep.tile([P, S], U8, name="x_scale", align_bytes=64)
+        def pos_at(n0, width):
+            g, in_piece = piece_of(POS_PIECES, n0)
+            return pos_sb[g][:, :, in_piece : in_piece + width]
+
+        x_scale = sbuf([P, S], U8, "x_scale")
         nc.vector.tensor_copy(x_scale[:], table_scales[:].indirect(offsets[:]))
         x_codes = []
 
-        def gather_words(g, tag):
+        def gather_words(g, takes_over=None):
             n0, n1 = GATHERS[g]
-            x_codes.append(keep.tile([P, n1 - n0], U32, name=f"x_codes{g}", tag=tag, align_bytes=64))
+            x_codes.append(sbuf([P, n1 - n0], U32, f"x_codes{g}", takes_over))
             nc.vector.tensor_copy(
                 x_codes[g][:],
                 table_words[:].bitcast(U32).indirect(offsets[:, n0 // PER_COLUMN : n1 // PER_COLUMN]),
             )
 
-        gather_words(0, "x_codes0")
+        gather_words(0)
 
-        w1_grouped = [
-            keep.tile([P, PACK, HALF, PACK], BF16, name=f"w1_grouped{half}", tag=f"w1_grouped{half}", align_bytes=64)
-            for half in range(2)
-        ]
-        w1_codes = keep.tile([P, H], U32, name="w1_codes", align_bytes=64)
-        w1_scale = keep.tile([P, H], U8, name="w1_scale", align_bytes=64)
-        for i, raw in enumerate(w1_raw):
+        w1_grouped = [sbuf([P, PACK, HALF, PACK], BF16, f"w1_grouped{half}") for half in range(2)]
+        w1_codes = sbuf([P, H], U32, "w1_codes")
+        w1_scale = sbuf([P, H], U8, "w1_scale")
+
+        def lay_out_w1(copy, i, t0, t1):
             half, m0 = divmod(i * W1_PIECE // PACK, HALF)
-            m1 = m0 + W1_PIECE // PACK
-            t_step = 2 if i == len(w1_raw) - 1 else PACK
-            for t0 in range(0, PACK, t_step):
-                copy = nc.vector.tensor_copy if t0 == 2 else nc.scalar.copy
-                copy(
-                    out=w1_grouped[half][:, t0 : t0 + t_step, m0:m1, :].rearrange("p t m j -> p m j t"),
-                    in_=raw[:].rearrange("p j (m t) -> p m j t", t=PACK)[:, :, :, t0 : t0 + t_step],
+            copy(
+                out=w1_grouped[half][:, t0:t1, m0 : m0 + W1_PIECE // PACK, :].rearrange("p t m j -> p m j t"),
+                in_=w1_raw[i][:].rearrange("p j (m t) -> p m j t", t=PACK)[:, :, :, t0:t1],
+            )
+
+        def quantise_w1(half):
+            for t in range(PACK):
+                cols = slice(t * P + half * HALF, t * P + (half + 1) * HALF)
+                nc.vector.quantize_mx(
+                    out=w1_codes[:, cols].bitcast(FP8X4),
+                    scales=w1_scale[:, cols],
+                    in_=w1_grouped[half][:, t, :, :].rearrange("p m j -> p (m j)"),
                 )
-            if m1 == HALF:
-                for t in range(PACK):
-                    cols = slice(t * P + half * HALF, t * P + (half + 1) * HALF)
-                    nc.vector.quantize_mx(
-                        out=w1_codes[:, cols].bitcast(FP8X4),
-                        scales=w1_scale[:, cols],
-                        in_=w1_grouped[half][:, t, :, :].rearrange("p m j -> p (m j)"),
-                    )
+
+        lay_out_w1(nc.scalar.copy, 0, 0, PACK)
+        lay_out_w1(nc.scalar.copy, 1, 0, PACK)
+        quantise_w1(0)
+        lay_out_w1(nc.scalar.copy, 2, 0, PACK)
+        lay_out_w1(nc.scalar.copy, 3, 0, 2)
+        lay_out_w1(nc.vector.tensor_copy, 3, 2, PACK)
+        quantise_w1(1)
 
         gather_words(1, "w1_raw3")
 
-        w2_grouped = keep.tile([P, N, PACK], BF16, name="w2_grouped", tag="w2_grouped", align_bytes=64)
-        w2_codes = keep.tile([P, N], U32, name="w2_codes", tag="pos1", align_bytes=64)
-        w2_scale = keep.tile([P, N], U8, name="w2_scale", align_bytes=64)
+        w2_grouped = sbuf([P, N, PACK], BF16, "w2_grouped")
+        w2_codes = sbuf([P, N], U32, "w2_codes", "pos0")
+        w2_scale = sbuf([P, N], U8, "w2_scale")
         nc.scalar.copy(
             out=w2_grouped[:].rearrange("p (c i) j -> p c j i", i=2),
             in_=w2_raw[:].rearrange("p j (c i) -> p c j i", i=2),
         )
 
-        def quantise_w2():
-            nc.vector.quantize_mx(
-                out=w2_codes[:].bitcast(FP8X4),
-                scales=w2_scale[:],
-                in_=w2_grouped[:].rearrange("p m j -> p (m j)"),
-            )
-
-        banks_used = []
+        first_banks = []
 
         def first_product(n0, width):
             gather, in_gather = piece_of(GATHERS, n0)
-            bank = hidden_banks.tile([P, PACK, width], F32, name="hidden_bank", tag=f"bank{len(banks_used) % HIDDEN_BANKS}")
-            banks_used.append(bank)
+            bank = hidden_banks.tile(
+                [P, PACK, width], F32, name="hidden_bank", tag=f"bank{len(first_banks) % HIDDEN_BANKS}"
+            )
+            first_banks.append(bank)
             for t in range(PACK):
                 nc.tensor.matmul_mx(
                     out=bank[:, t, :],
@@ -151,22 +157,23 @@ def tile_picked_embpos_none_p_kernel(tc, x_words, x_scales, w1, w2, pos, offs, o
                 )
             return bank
 
-        def add_pos(n0, width, target):
-            g, in_pos = piece_of(POS_PIECES, n0)
-            bank = first_product(n0, width)
+        def add_pos(hidden, product, n0, width):
             nc.vector.tensor_tensor(
-                out=target.rearrange("p (c i) t -> p c t i", i=2),
-                in0=bank[:].rearrange("p t (c i) -> p c t i", i=2),
-                in1=pos_sb[g][:, :, in_pos : in_pos + width].rearrange("p t (c i) -> p c t i", i=2),
+                out=hidden.rearrange("p (c i) t -> p c t i", i=2),
+                in0=product.rearrange("p t (c i) -> p c t i", i=2),
+                in1=pos_at(n0, width).rearrange("p t (c i) -> p c t i", i=2),
                 op=ADD,
             )
+
+        def first_layer(hidden, n0, width):
+            add_pos(hidden, first_product(n0, width)[:], n0, width)
 
         def quantise(codes, scale, values):
             nc.vector.quantize_mx(out=codes.bitcast(FP8X4), scales=scale, in_=values.rearrange("p n t -> p (n t)"))
 
-        def second_product(product, b, codes, scale):
+        def second_product(bank, b, codes, scale):
             nc.tensor.matmul_mx(
-                out=product,
+                out=bank,
                 lhsT=w2_codes[:, b * P : (b + 1) * P].bitcast(FP8X4),
                 lhsT_scale=w2_scale[:, b * P : (b + 1) * P],
                 rhs=codes.bitcast(FP8X4),
@@ -177,91 +184,91 @@ def tile_picked_embpos_none_p_kernel(tc, x_words, x_scales, w1, w2, pos, offs, o
 
         out_rows = out.rearrange("(b p) n -> p b n", p=P)
 
-        def second_layer(codes, scale, width, targets, copies):
-            for b in range(2):
-                product = out_banks.tile([P, width], F32, name="out_bank")
-                second_product(product[:], b, codes, scale)
-                copies[b](out=targets[b], in_=product[:])
+        def second_layer(result, codes, scale, width):
+            for b in range(OUT_TILES):
+                bank = out_banks.tile([P, width], F32, name="out_bank")
+                second_product(bank[:], b, codes, scale)
+                nc.scalar.copy(out=result[:, b, :], in_=bank[:])
 
-        def sbuf(shape, dtype, name, tag=None):
-            return keep.tile(shape, dtype, name=name, tag=tag or name, align_bytes=64)
-
-        scalar_only = (nc.scalar.copy, nc.scalar.copy)
-        both = (nc.scalar.copy, nc.vector.tensor_copy)
         h_scale = sbuf([P, S], U8, "h_scale")
 
-        hidden0 = sbuf([P, 256, PACK], BF16, "hidden0")
-        hidden1 = sbuf([P, 128, PACK], BF16, "hidden1")
-        add_pos(0, 128, hidden0[:, :128, :])
-        add_pos(128, 128, hidden0[:, 128:, :])
-        add_pos(256, 128, hidden1[:])
-        bank = first_product(384, 128)
-        shared_bank = bank
-        product = shared.tile([P, GP, PACK], F32, name="product", offset=0, align_bytes=64)
-        nc.scalar.copy(out=product[:], in_=bank[:, :, :GP].rearrange("p t n -> p n t"))
-        codes0 = sbuf([P, 384], U32, "codes0")
-        quantise(codes0[:, :256], h_scale[:, 0:256], hidden0[:])
-        quantise(codes0[:, 256:], h_scale[:, 256:384], hidden1[:])
-        quantise_w2()
-        hidden2 = sbuf([P, 128, PACK], BF16, "hidden2", "w2_grouped")
-        nc.gpsimd.tensor_tensor(
-            out=hidden2[:, :GP, :], in0=product[:], in1=pos_sb[2][:, :, :GP].rearrange("p t n -> p n t"), op=ADD
+        hidden_0 = sbuf([P, 2 * CHUNK, PACK], BF16, "hidden_0")
+        hidden_256 = sbuf([P, CHUNK, PACK], BF16, "hidden_256")
+        first_layer(hidden_0[:, :CHUNK, :], 0, CHUNK)
+        first_layer(hidden_0[:, CHUNK:, :], 128, CHUNK)
+        first_layer(hidden_256[:], 256, CHUNK)
+        shared_bank = first_product(384, CHUNK)
+        on_gpsimd = slice(CHUNK - GPSIMD_ENTRIES, CHUNK)
+        on_vector = slice(0, CHUNK - GPSIMD_ENTRIES)
+        gpsimd_product = behind_gpsimd.tile(
+            [P, GPSIMD_ENTRIES, PACK], F32, name="gpsimd_product", offset=0, align_bytes=64
         )
-        result0 = sbuf([P, 2, 384], F32, "result0")
-        second_layer(codes0[:, :256], h_scale[:, 0:256], 256, [result0[:, b, :256] for b in range(2)], scalar_only)
-        second_layer(codes0[:, 256:], h_scale[:, 256:384], 128, [result0[:, b, 256:] for b in range(2)], scalar_only)
-        nc.sync.dma_start(out=out_rows[:, :, 0:384], in_=result0[:])
+        nc.scalar.copy(out=gpsimd_product[:], in_=shared_bank[:, :, on_gpsimd].rearrange("p t n -> p n t"))
+        codes_0 = sbuf([P, 3 * CHUNK], U32, "codes_0")
+        quantise(codes_0[:, :256], h_scale[:, 0:256], hidden_0[:])
+        quantise(codes_0[:, 256:], h_scale[:, 256:384], hidden_256[:])
+        quantise(w2_codes[:], w2_scale[:], w2_grouped[:])
 
-        hidden3 = sbuf([P, 256, PACK], BF16, "hidden3")
-        hidden4 = sbuf([P, 128, PACK], BF16, "hidden4")
-        add_pos(512, 128, hidden3[:, :128, :])
-        nc.vector.tensor_tensor(
-            out=hidden2[:, GP:, :].rearrange("p (c i) t -> p c t i", i=2),
-            in0=shared_bank[:, :, GP:].rearrange("p t (c i) -> p c t i", i=2),
-            in1=pos_sb[2][:, :, GP:128].rearrange("p t (c i) -> p c t i", i=2),
+        hidden_384 = sbuf([P, CHUNK, PACK], BF16, "hidden_384", "w2_grouped")
+        nc.gpsimd.tensor_tensor(
+            out=hidden_384[:, on_gpsimd, :],
+            in0=gpsimd_product[:],
+            in1=pos_at(384 + on_gpsimd.start, GPSIMD_ENTRIES).rearrange("p t n -> p n t"),
             op=ADD,
         )
-        add_pos(640, 128, hidden3[:, 128:, :])
-        add_pos(768, 128, hidden4[:])
+        result_0 = sbuf([P, OUT_TILES, 3 * CHUNK], F32, "result_0")
+        second_layer(result_0[:, :, :256], codes_0[:, :256], h_scale[:, 0:256], 2 * CHUNK)
+        second_layer(result_0[:, :, 256:], codes_0[:, 256:], h_scale[:, 256:384], CHUNK)
+        nc.sync.dma_start(out=out_rows[:, :, 0:384], in_=result_0[:])
 
-        codes2 = sbuf([P, 128], U32, "codes2")
-        quantise(codes2[:], h_scale[:, 384:512], hidden2[:])
-        result2 = sbuf([P, 2, 128], F32, "result2")
-        second_layer(codes2[:], h_scale[:, 384:512], 128, [result2[:, b, :] for b in range(2)], scalar_only)
-        nc.sync.dma_start(out=out_rows[:, :, 384:512], in_=result2[:])
+        hidden_512 = sbuf([P, 2 * CHUNK, PACK], BF16, "hidden_512")
+        hidden_768 = sbuf([P, CHUNK, PACK], BF16, "hidden_768")
+        add_pos(hidden_384[:, on_vector, :], shared_bank[:, :, on_vector], 384, CHUNK - GPSIMD_ENTRIES)
+        first_layer(hidden_512[:, :CHUNK, :], 512, CHUNK)
+        first_layer(hidden_512[:, CHUNK:, :], 640, CHUNK)
+        first_layer(hidden_768[:], 768, CHUNK)
 
-        codes3 = shared.tile([P, 256], U32, name="codes3", offset=0, align_bytes=64)
-        quantise(codes3[:], h_scale[:, 512:768], hidden3[:])
-        for b in range(2):
-            bank = out_banks.tile([P, 256], F32, name="out_bank")
-            second_product(bank[:], b, codes3[:], h_scale[:, 512:768])
-            part = sbuf([P, 256], F32, f"part{b}")
+        codes_384 = sbuf([P, CHUNK], U32, "codes_384")
+        quantise(codes_384[:], h_scale[:, 384:512], hidden_384[:])
+        result_384 = sbuf([P, OUT_TILES, CHUNK], F32, "result_384")
+        second_layer(result_384[:], codes_384[:], h_scale[:, 384:512], CHUNK)
+        nc.sync.dma_start(out=out_rows[:, :, 384:512], in_=result_384[:])
+
+        codes_512 = behind_gpsimd.tile([P, 2 * CHUNK], U32, name="codes_512", offset=0, align_bytes=64)
+        quantise(codes_512[:], h_scale[:, 512:768], hidden_512[:])
+        for b in range(OUT_TILES):
+            bank = out_banks.tile([P, 2 * CHUNK], F32, name="out_bank")
+            second_product(bank[:], b, codes_512[:], h_scale[:, 512:768])
+            part = sbuf([P, 2 * CHUNK], F32, f"result_512_{b}")
             nc.scalar.copy(out=part[:], in_=bank[:])
             nc.sync.dma_start(out=out_rows[:, b, 512:768], in_=part[:])
 
-        hidden5 = shared.tile([P, 64, PACK], BF16, name="hidden5", offset=1024, align_bytes=64)
-        add_pos(896, 64, hidden5[:])
-        codes4 = sbuf([P, 128], U32, "codes4", "pos2")
-        quantise(codes4[:], h_scale[:, 768:896], hidden4[:])
-        hidden6 = sbuf([P, 64, PACK], BF16, "hidden6", "hidden3")
-        add_pos(960, 64, hidden6[:])
-        codes5 = sbuf([P, 128], U32, "codes5", "product_late")
-        quantise(codes5[:, :64], h_scale[:, 896:960], hidden5[:])
-        quantise(codes5[:, 64:], h_scale[:, 960:1024], hidden6[:])
+        hidden_896 = behind_gpsimd.tile([P, LAST_HALF, PACK], BF16, name="hidden_896", offset=1024, align_bytes=64)
+        first_layer(hidden_896[:], 896, LAST_HALF)
+        codes_768 = sbuf([P, CHUNK], U32, "codes_768", f"pos{GPSIMD_PIECE}")
+        quantise(codes_768[:], h_scale[:, 768:896], hidden_768[:])
+        hidden_960 = sbuf([P, LAST_HALF, PACK], BF16, "hidden_960", "hidden_512")
+        first_layer(hidden_960[:], 960, LAST_HALF)
+        codes_896 = sbuf([P, CHUNK], U32, "codes_896")
+        quantise(codes_896[:, :LAST_HALF], h_scale[:, 896:960], hidden_896[:])
+        quantise(codes_896[:, LAST_HALF:], h_scale[:, 960:1024], hidden_960[:])
 
-        result4 = sbuf([P, 2, 128], F32, "result4")
-        banks4 = [hidden_banks.tile([P, 128], F32, name="late_bank", tag=f"bank{b + 1}") for b in range(2)]
-        for b in range(2):
-            second_product(banks4[b][:], b, codes4[:], h_scale[:, 768:896])
-        for b in range(2):
-            scalar_only[b](out=result4[:, b, :], in_=banks4[b][:])
-        nc.sync.dma_start(out=out_rows[:, :, 768:896], in_=result4[:])
+        result_768 = sbuf([P, OUT_TILES, CHUNK], F32, "result_768")
+        banks_768 = [
+            hidden_banks.tile([P, CHUNK], F32, name="late_bank", tag=f"bank{b + 1}") for b in range(OUT_TILES)
+        ]
+        for b in range(OUT_TILES):
+            second_product(banks_768[b][:], b, codes_768[:], h_scale[:, 768:896])
+        for b in range(OUT_TILES):
+            nc.scalar.copy(out=result_768[:, b, :], in_=banks_768[b][:])
+        nc.sync.dma_start(out=out_rows[:, :, 768:896], in_=result_768[:])
 
-        result5 = sbuf([P, 2, 128], F32, "result5")
-        banks5 = [out_banks.tile([P, 128], F32, name="out_bank") for b in range(2)]
-        for c in (0, 64):
-            for b in range(2):
-                second_product(banks5[b][:, c : c + 64], b, codes5[:, c : c + 64], h_scale[:, 896 + c : 960 + c])
-        for b in range(2):
-            both[b](out=result5[:, b, :], in_=banks5[b][:])
-        nc.sync.dma_start(out=out_rows[:, :, 896:1024], in_=result5[:])
+        result_896 = sbuf([P, OUT_TILES, CHUNK], F32, "result_896")
+        banks_896 = [out_banks.tile([P, CHUNK], F32, name="out_bank") for b in range(OUT_TILES)]
+        for c in range(0, CHUNK, LAST_HALF):
+            cols = slice(c, c + LAST_HALF)
+            for b in range(OUT_TILES):
+                second_product(banks_896[b][:, cols], b, codes_896[:, cols], h_scale[:, 896 + c : 896 + c + LAST_HALF])
+        nc.scalar.copy(out=result_896[:, 0, :], in_=banks_896[0][:])
+        nc.vector.tensor_copy(out=result_896[:, 1, :], in_=banks_896[1][:])
+        nc.sync.dma_start(out=out_rows[:, :, 896:1024], in_=result_896[:])

@@ -23,7 +23,7 @@ OUT_BANKS = 4
 OUT_TILES = N // P
 HALF = 64
 
-FIRST_WORDS = 768
+FIRST_WORDS = 512
 W1_PIECE = 128
 GATHERS = ((0, 512), (512, 1024))
 GPSIMD_ENTRIES = 96

@@ -23,7 +23,7 @@ OUT_BANKS = 4
 OUT_TILES = N // P
 HALF = 64
 
-FIRST_WORDS = 512
+FIRST_WORDS = 768
 W1_PIECE = 128
 GATHERS = ((0, 512), (512, 1024))
 GPSIMD_ENTRIES = 96
@@ -254,21 +254,20 @@ def tile_picked_embpos_none_p_kernel(tc, x_words, x_scales, w1, w2, pos, offs, o
         quantise(codes_896[:, LAST_HALF:], h_scale[:, 960:1024], hidden_960[:])
 
         result_768 = sbuf([P, OUT_TILES, CHUNK], F32, "result_768")
-        banks_768 = [
-            hidden_banks.tile([P, CHUNK], F32, name="late_bank", tag=f"bank{b + 1}") for b in range(OUT_TILES)
-        ]
+        bank_768 = hidden_banks.tile([P, OUT_TILES, CHUNK], F32, name="bank_768", tag="bank1")
         for b in range(OUT_TILES):
-            second_product(banks_768[b][:], b, codes_768[:], h_scale[:, 768:896])
-        for b in range(OUT_TILES):
-            nc.scalar.copy(out=result_768[:, b, :], in_=banks_768[b][:])
+            second_product(bank_768[:, b, :], b, codes_768[:], h_scale[:, 768:896])
+        nc.scalar.copy(out=result_768[:], in_=bank_768[:])
         nc.sync.dma_start(out=out_rows[:, :, 768:896], in_=result_768[:])
 
         result_896 = sbuf([P, OUT_TILES, CHUNK], F32, "result_896")
-        banks_896 = [out_banks.tile([P, CHUNK], F32, name="out_bank") for b in range(OUT_TILES)]
-        for c in range(0, CHUNK, LAST_HALF):
-            cols = slice(c, c + LAST_HALF)
-            for b in range(OUT_TILES):
-                second_product(banks_896[b][:, cols], b, codes_896[:, cols], h_scale[:, 896 + c : 896 + c + LAST_HALF])
-        nc.scalar.copy(out=result_896[:, 0, :], in_=banks_896[0][:])
-        nc.vector.tensor_copy(out=result_896[:, 1, :], in_=banks_896[1][:])
+        bank_896 = hidden_banks.tile([P, OUT_TILES, LAST_HALF], F32, name="bank_896", tag="bank2")
+        for b in range(OUT_TILES):
+            second_product(bank_896[:, b, :], b, codes_896[:, :LAST_HALF], h_scale[:, 896:960])
+        nc.scalar.copy(out=result_896[:, :, :LAST_HALF], in_=bank_896[:])
+        banks_960 = [out_banks.tile([P, LAST_HALF], F32, name="out_bank") for b in range(OUT_TILES)]
+        for b in range(OUT_TILES):
+            second_product(banks_960[b][:], b, codes_896[:, LAST_HALF:], h_scale[:, 960:1024])
+        nc.scalar.copy(out=result_896[:, 0, LAST_HALF:], in_=banks_960[0][:])
+        nc.vector.tensor_copy(out=result_896[:, 1, LAST_HALF:], in_=banks_960[1][:])
         nc.sync.dma_start(out=out_rows[:, :, 896:1024], in_=result_896[:])

@@ -27,10 +27,15 @@ FIRST_WORDS = 768
 W1_PIECE = 128
 GATHERS = ((0, 512), (512, 1024))
 GPSIMD_ENTRIES = 96
-POS_PIECES = ((0, 256), (256, 416), (416, 640), (640, 768), (768, 896), (896, 1024))
+POS_PIECES = ((0, 256), (256, 512)) + tuple((n0, n0 + CHUNK) for n0 in range(512, S, CHUNK))
 W2_PIECE = 1
-GPSIMD_PIECE = 2
 LAST_HALF = CHUNK // 2
+
+W2_AT = 0
+SECOND_CHUNK_AT = 2048
+ACROSS_BOTH_AT = 1536
+PRODUCT_AT = 4096
+PRODUCT_END_AT = 5120
 
 
 def piece_of(pieces, n0):
@@ -48,6 +53,9 @@ def tile_picked_embpos_none_p_kernel(tc, x_words, x_scales, w1, w2, pos, offs, o
 
         def sbuf(shape, dtype, name, takes_over=None):
             return keep.tile(shape, dtype, name=name, tag=takes_over or name, align_bytes=64)
+
+        def placed(shape, dtype, name, offset):
+            return behind_gpsimd.tile(shape, dtype, name=name, offset=offset, align_bytes=64)
 
         offsets = keep.tile([P, S // PER_COLUMN], U16, name="offsets")
         nc.sync.dma_start(offsets[:], offs)
@@ -129,8 +137,8 @@ def tile_picked_embpos_none_p_kernel(tc, x_words, x_scales, w1, w2, pos, offs, o
 
         gather_words(1, "w1_raw3")
 
-        w2_grouped = sbuf([P, N, PACK], BF16, "w2_grouped")
-        w2_codes = sbuf([P, N], U32, "w2_codes", "pos0")
+        w2_grouped = placed([P, N, PACK], BF16, "w2_grouped", W2_AT)
+        w2_codes = sbuf([P, N], U32, "w2_codes")
         w2_scale = sbuf([P, N], U8, "w2_scale")
         nc.scalar.copy(
             out=w2_grouped[:].rearrange("p (c i) j -> p c j i", i=2),
@@ -192,62 +200,65 @@ def tile_picked_embpos_none_p_kernel(tc, x_words, x_scales, w1, w2, pos, offs, o
 
         h_scale = sbuf([P, S], U8, "h_scale")
 
-        hidden_0 = sbuf([P, 2 * CHUNK, PACK], BF16, "hidden_0")
-        hidden_256 = sbuf([P, CHUNK, PACK], BF16, "hidden_256")
-        first_layer(hidden_0[:, :CHUNK, :], 0, CHUNK)
-        first_layer(hidden_0[:, CHUNK:, :], 128, CHUNK)
-        first_layer(hidden_256[:], 256, CHUNK)
-        shared_bank = first_product(384, CHUNK)
+        def leave_pair(codes, n0):
+            result = sbuf([P, OUT_TILES, 2 * CHUNK], F32, f"result_{n0}")
+            second_layer(result[:], codes, h_scale[:, n0 : n0 + 2 * CHUNK], 2 * CHUNK)
+            nc.sync.dma_start(out=out_rows[:, :, n0 : n0 + 2 * CHUNK], in_=result[:])
+
+        def leave_chunk(codes, n0):
+            bank = out_banks.tile([P, OUT_TILES, CHUNK], F32, name="out_bank")
+            for b in range(OUT_TILES):
+                second_product(bank[:, b, :], b, codes, h_scale[:, n0 : n0 + CHUNK])
+            result = sbuf([P, OUT_TILES, CHUNK], F32, f"result_{n0}")
+            nc.scalar.copy(out=result[:], in_=bank[:])
+            nc.sync.dma_start(out=out_rows[:, :, n0 : n0 + CHUNK], in_=result[:])
+
+        hidden_0 = sbuf([P, CHUNK, PACK], BF16, "hidden_0")
+        hidden_128 = placed([P, CHUNK, PACK], BF16, "hidden_128", SECOND_CHUNK_AT)
+        first_layer(hidden_0[:], 0, CHUNK)
+        first_layer(hidden_128[:], 128, CHUNK)
+        shared_bank = first_product(256, CHUNK)
         on_gpsimd = slice(CHUNK - GPSIMD_ENTRIES, CHUNK)
         on_vector = slice(0, CHUNK - GPSIMD_ENTRIES)
-        gpsimd_product = behind_gpsimd.tile(
-            [P, GPSIMD_ENTRIES, PACK], F32, name="gpsimd_product", offset=0, align_bytes=64
-        )
+        gpsimd_product = placed([P, GPSIMD_ENTRIES, PACK], F32, "gpsimd_product", PRODUCT_AT)
         nc.scalar.copy(out=gpsimd_product[:], in_=shared_bank[:, :, on_gpsimd].rearrange("p t n -> p n t"))
-        codes_0 = sbuf([P, 3 * CHUNK], U32, "codes_0")
-        quantise(codes_0[:, :256], h_scale[:, 0:256], hidden_0[:])
-        quantise(codes_0[:, 256:], h_scale[:, 256:384], hidden_256[:])
+        codes_0 = sbuf([P, 2 * CHUNK], U32, "codes_0")
+        quantise(codes_0[:, :CHUNK], h_scale[:, 0:128], hidden_0[:])
+        quantise(codes_0[:, CHUNK:], h_scale[:, 128:256], hidden_128[:])
         quantise(w2_codes[:], w2_scale[:], w2_grouped[:])
 
-        hidden_384 = sbuf([P, CHUNK, PACK], BF16, "hidden_384", "w2_grouped")
+        hidden_256 = placed([P, CHUNK, PACK], BF16, "hidden_256", ACROSS_BOTH_AT)
         nc.gpsimd.tensor_tensor(
-            out=hidden_384[:, on_gpsimd, :],
+            out=hidden_256[:, on_gpsimd, :],
             in0=gpsimd_product[:],
-            in1=pos_at(384 + on_gpsimd.start, GPSIMD_ENTRIES).rearrange("p t n -> p n t"),
+            in1=pos_at(256 + on_gpsimd.start, GPSIMD_ENTRIES).rearrange("p t n -> p n t"),
             op=ADD,
         )
-        result_0 = sbuf([P, OUT_TILES, 3 * CHUNK], F32, "result_0")
-        second_layer(result_0[:, :, :256], codes_0[:, :256], h_scale[:, 0:256], 2 * CHUNK)
-        second_layer(result_0[:, :, 256:], codes_0[:, 256:], h_scale[:, 256:384], CHUNK)
-        nc.sync.dma_start(out=out_rows[:, :, 0:384], in_=result_0[:])
+        leave_pair(codes_0[:], 0)
 
+        hidden_384 = sbuf([P, CHUNK, PACK], BF16, "hidden_384", "hidden_0")
         hidden_512 = sbuf([P, 2 * CHUNK, PACK], BF16, "hidden_512")
-        hidden_768 = sbuf([P, CHUNK, PACK], BF16, "hidden_768")
-        add_pos(hidden_384[:, on_vector, :], shared_bank[:, :, on_vector], 384, CHUNK - GPSIMD_ENTRIES)
+        first_layer(hidden_384[:], 384, CHUNK)
+        add_pos(hidden_256[:, on_vector, :], shared_bank[:, :, on_vector], 256, CHUNK - GPSIMD_ENTRIES)
         first_layer(hidden_512[:, :CHUNK, :], 512, CHUNK)
         first_layer(hidden_512[:, CHUNK:, :], 640, CHUNK)
-        first_layer(hidden_768[:], 768, CHUNK)
 
-        codes_384 = sbuf([P, CHUNK], U32, "codes_384")
-        quantise(codes_384[:], h_scale[:, 384:512], hidden_384[:])
-        result_384 = sbuf([P, OUT_TILES, CHUNK], F32, "result_384")
-        second_layer(result_384[:], codes_384[:], h_scale[:, 384:512], CHUNK)
-        nc.sync.dma_start(out=out_rows[:, :, 384:512], in_=result_384[:])
-
-        codes_512 = behind_gpsimd.tile([P, 2 * CHUNK], U32, name="codes_512", offset=0, align_bytes=64)
+        codes_256 = placed([P, 2 * CHUNK], U32, "codes_256", PRODUCT_AT)
+        codes_512 = placed([P, 2 * CHUNK], U32, "codes_512", PRODUCT_END_AT)
+        quantise(codes_256[:, :CHUNK], h_scale[:, 256:384], hidden_256[:])
+        leave_chunk(codes_256[:, :CHUNK], 256)
+        quantise(codes_256[:, CHUNK:], h_scale[:, 384:512], hidden_384[:])
+        leave_chunk(codes_256[:, CHUNK:], 384)
         quantise(codes_512[:], h_scale[:, 512:768], hidden_512[:])
-        for b in range(OUT_TILES):
-            bank = out_banks.tile([P, 2 * CHUNK], F32, name="out_bank")
-            second_product(bank[:], b, codes_512[:], h_scale[:, 512:768])
-            part = sbuf([P, 2 * CHUNK], F32, f"result_512_{b}")
-            nc.scalar.copy(out=part[:], in_=bank[:])
-            nc.sync.dma_start(out=out_rows[:, b, 512:768], in_=part[:])
+        leave_pair(codes_512[:], 512)
 
-        hidden_896 = behind_gpsimd.tile([P, LAST_HALF, PACK], BF16, name="hidden_896", offset=1024, align_bytes=64)
+        hidden_768 = placed([P, CHUNK, PACK], BF16, "hidden_768", ACROSS_BOTH_AT)
+        first_layer(hidden_768[:], 768, CHUNK)
+        hidden_896 = sbuf([P, LAST_HALF, PACK], BF16, "hidden_896", "hidden_512")
         first_layer(hidden_896[:], 896, LAST_HALF)
-        codes_768 = sbuf([P, CHUNK], U32, "codes_768", f"pos{GPSIMD_PIECE}")
+        codes_768 = sbuf([P, CHUNK], U32, "codes_768")
         quantise(codes_768[:], h_scale[:, 768:896], hidden_768[:])
-        hidden_960 = sbuf([P, LAST_HALF, PACK], BF16, "hidden_960", "hidden_512")
+        hidden_960 = sbuf([P, LAST_HALF, PACK], BF16, "hidden_960", "hidden_0")
         first_layer(hidden_960[:], 960, LAST_HALF)
         codes_896 = sbuf([P, CHUNK], U32, "codes_896")
         quantise(codes_896[:, :LAST_HALF], h_scale[:, 896:960], hidden_896[:])

@@ -68,8 +68,7 @@ def tile_picked_embpos_none_p_kernel(tc, x_words, x_scales, w1, w2, pos, offs, o
         word_rows = x_words[0].rearrange("p n t -> p (n t)").bitcast(I32)
         nc.sync.dma_start(out=table_words[:, :FIRST_WORDS], in_=word_rows[:, :FIRST_WORDS])
         for r in range(4):
-            queue = nc.sync if r % 2 == 0 else nc.scalar
-            queue.dma_start(
+            nc.sync.dma_start(
                 out=table_scales[r:P:32, :].bitcast(I32),
                 in_=x_scales[0][r:16:4, :].bitcast(I32),
             )

@@ -26,7 +26,7 @@ HALF = 64
 FIRST_WORDS = 768
 W1_PIECE = 128
 GATHERS = ((0, 512), (512, 1024))
-GPSIMD_ENTRIES = 96
+GPSIMD_ENTRIES = 80
 POS_PIECES = ((0, 256), (256, 512)) + tuple((n0, n0 + CHUNK) for n0 in range(512, S, CHUNK))
 W2_PIECE = 1
 LAST_HALF = CHUNK // 2

@@ -52,12 +52,12 @@ def tile_picked_embpos_none_p_kernel(tc, x_words, x_scales, w1, w2, pos, offs, o
         out_banks = ctx.enter_context(tc.psum_pool(name="out_banks", bufs=OUT_BANKS))
 
         def sbuf(shape, dtype, name, takes_over=None):
-            return keep.tile(shape, dtype, name=name, tag=takes_over or name, align_bytes=64)
+            return keep.tile(shape, dtype, name=name, tag=takes_over or name, align_bytes=256)
 
         def placed(shape, dtype, name, offset):
-            return behind_gpsimd.tile(shape, dtype, name=name, offset=offset, align_bytes=64)
+            return behind_gpsimd.tile(shape, dtype, name=name, offset=offset, align_bytes=256)
 
-        offsets = keep.tile([P, S // PER_COLUMN], U16, name="offsets")
+        offsets = keep.tile([P, S // PER_COLUMN], U16, name="offsets", align_bytes=256)
         nc.sync.dma_start(offsets[:], offs)
 
         w1_raw = [sbuf([P, PACK, W1_PIECE], F32, f"w1_raw{i}") for i in range(H // W1_PIECE)]

@@ -26,14 +26,15 @@ HALF = 64
 FIRST_WORDS = 768
 W1_PIECE = 128
 GATHERS = ((0, 512), (512, 1024))
-GPSIMD_ENTRIES = 80
+GPSIMD_ENTRIES = 96
 POS_PIECES = ((0, 256), (256, 512)) + tuple((n0, n0 + CHUNK) for n0 in range(512, S, CHUNK))
 W2_PIECE = 1
 LAST_HALF = CHUNK // 2
 
 W2_AT = 0
-SECOND_CHUNK_AT = 2048
+FIRST_PAIR_AT = 2048
 ACROSS_BOTH_AT = 1536
+ON_FIRST_PAIR_AT = 3072
 PRODUCT_AT = 4096
 PRODUCT_END_AT = 5120
 
@@ -139,10 +140,11 @@ def tile_picked_embpos_none_p_kernel(tc, x_words, x_scales, w1, w2, pos, offs, o
         w2_grouped = placed([P, N, PACK], BF16, "w2_grouped", W2_AT)
         w2_codes = sbuf([P, N], U32, "w2_codes")
         w2_scale = sbuf([P, N], U8, "w2_scale")
-        nc.scalar.copy(
-            out=w2_grouped[:].rearrange("p (c i) j -> p c j i", i=2),
-            in_=w2_raw[:].rearrange("p j (c i) -> p c j i", i=2),
-        )
+        for b in range(OUT_TILES):
+            nc.scalar.copy(
+                out=w2_grouped[:, b * P : (b + 1) * P, :].rearrange("p (c i) j -> p c j i", i=2),
+                in_=w2_raw[:, :, b * P : (b + 1) * P].rearrange("p j (c i) -> p c j i", i=2),
+            )
 
         first_banks = []
 
@@ -204,27 +206,27 @@ def tile_picked_embpos_none_p_kernel(tc, x_words, x_scales, w1, w2, pos, offs, o
             second_layer(result[:], codes, h_scale[:, n0 : n0 + 2 * CHUNK], 2 * CHUNK)
             nc.sync.dma_start(out=out_rows[:, :, n0 : n0 + 2 * CHUNK], in_=result[:])
 
-        def leave_chunk(codes, n0):
-            bank = out_banks.tile([P, OUT_TILES, CHUNK], F32, name="out_bank")
+        def leave_chunk(codes, n0, width=CHUNK):
+            bank = out_banks.tile([P, OUT_TILES, width], F32, name="out_bank")
             for b in range(OUT_TILES):
-                second_product(bank[:, b, :], b, codes, h_scale[:, n0 : n0 + CHUNK])
-            result = sbuf([P, OUT_TILES, CHUNK], F32, f"result_{n0}")
+                second_product(bank[:, b, :], b, codes, h_scale[:, n0 : n0 + width])
+            result = sbuf([P, OUT_TILES, width], F32, f"result_{n0}")
             nc.scalar.copy(out=result[:], in_=bank[:])
-            nc.sync.dma_start(out=out_rows[:, :, n0 : n0 + CHUNK], in_=result[:])
+            nc.sync.dma_start(out=out_rows[:, :, n0 : n0 + width], in_=result[:])
 
-        hidden_0 = sbuf([P, CHUNK, PACK], BF16, "hidden_0")
-        hidden_128 = placed([P, CHUNK, PACK], BF16, "hidden_128", SECOND_CHUNK_AT)
-        first_layer(hidden_0[:], 0, CHUNK)
-        first_layer(hidden_128[:], 128, CHUNK)
+        hidden_0 = placed([P, 2 * CHUNK, PACK], BF16, "hidden_0", FIRST_PAIR_AT)
+        first_layer(hidden_0[:, :CHUNK, :], 0, CHUNK)
+        first_layer(hidden_0[:, CHUNK:, :], 128, CHUNK)
         shared_bank = first_product(256, CHUNK)
         on_gpsimd = slice(CHUNK - GPSIMD_ENTRIES, CHUNK)
         on_vector = slice(0, CHUNK - GPSIMD_ENTRIES)
         gpsimd_product = placed([P, GPSIMD_ENTRIES, PACK], F32, "gpsimd_product", PRODUCT_AT)
         nc.scalar.copy(out=gpsimd_product[:], in_=shared_bank[:, :, on_gpsimd].rearrange("p t n -> p n t"))
         codes_0 = sbuf([P, 2 * CHUNK], U32, "codes_0")
-        quantise(codes_0[:, :CHUNK], h_scale[:, 0:128], hidden_0[:])
-        quantise(codes_0[:, CHUNK:], h_scale[:, 128:256], hidden_128[:])
-        quantise(w2_codes[:], w2_scale[:], w2_grouped[:])
+        quantise(codes_0[:, :CHUNK], h_scale[:, 0:128], hidden_0[:, :CHUNK, :])
+        quantise(w2_codes[:, :P], w2_scale[:, :P], w2_grouped[:, :P, :])
+        quantise(codes_0[:, CHUNK:], h_scale[:, 128:256], hidden_0[:, CHUNK:, :])
+        quantise(w2_codes[:, P:], w2_scale[:, P:], w2_grouped[:, P:, :])
 
         hidden_256 = placed([P, CHUNK, PACK], BF16, "hidden_256", ACROSS_BOTH_AT)
         nc.gpsimd.tensor_tensor(
@@ -233,9 +235,9 @@ def tile_picked_embpos_none_p_kernel(tc, x_words, x_scales, w1, w2, pos, offs, o
             in1=pos_at(256 + on_gpsimd.start, GPSIMD_ENTRIES).rearrange("p t n -> p n t"),
             op=ADD,
         )
-        leave_pair(codes_0[:], 0)
+        leave_chunk(codes_0[:], 0, 2 * CHUNK)
 
-        hidden_384 = sbuf([P, CHUNK, PACK], BF16, "hidden_384", "hidden_0")
+        hidden_384 = placed([P, CHUNK, PACK], BF16, "hidden_384", ON_FIRST_PAIR_AT)
         hidden_512 = sbuf([P, 2 * CHUNK, PACK], BF16, "hidden_512")
         first_layer(hidden_384[:], 384, CHUNK)
         add_pos(hidden_256[:, on_vector, :], shared_bank[:, :, on_vector], 256, CHUNK - GPSIMD_ENTRIES)
@@ -257,7 +259,7 @@ def tile_picked_embpos_none_p_kernel(tc, x_words, x_scales, w1, w2, pos, offs, o
         first_layer(hidden_896[:], 896, LAST_HALF)
         codes_768 = sbuf([P, CHUNK], U32, "codes_768")
         quantise(codes_768[:], h_scale[:, 768:896], hidden_768[:])
-        hidden_960 = sbuf([P, LAST_HALF, PACK], BF16, "hidden_960", "hidden_0")
+        hidden_960 = sbuf([P, LAST_HALF, PACK], BF16, "hidden_960")
         first_layer(hidden_960[:], 960, LAST_HALF)
         codes_896 = sbuf([P, CHUNK], U32, "codes_896")
         quantise(codes_896[:, :LAST_HALF], h_scale[:, 896:960], hidden_896[:])

@@ -277,9 +277,8 @@ def tile_picked_embpos_none_p_kernel(tc, x_words, x_scales, w1, w2, pos, offs, o
         for b in range(OUT_TILES):
             second_product(bank_896[:, b, :], b, codes_896[:, :LAST_HALF], h_scale[:, 896:960])
         nc.scalar.copy(out=result_896[:, :, :LAST_HALF], in_=bank_896[:])
-        banks_960 = [out_banks.tile([P, LAST_HALF], F32, name="out_bank") for b in range(OUT_TILES)]
+        bank_960 = out_banks.tile([P, OUT_TILES, LAST_HALF], F32, name="out_bank")
         for b in range(OUT_TILES):
-            second_product(banks_960[b][:], b, codes_896[:, LAST_HALF:], h_scale[:, 960:1024])
-        nc.scalar.copy(out=result_896[:, 0, LAST_HALF:], in_=banks_960[0][:])
-        nc.vector.tensor_copy(out=result_896[:, 1, LAST_HALF:], in_=banks_960[1][:])
+            second_product(bank_960[:, b, :], b, codes_896[:, LAST_HALF:], h_scale[:, 960:1024])
+        nc.scalar.copy(out=result_896[:, :, LAST_HALF:], in_=bank_960[:])
         nc.sync.dma_start(out=out_rows[:, :, 896:1024], in_=result_896[:])

from contextlib import ExitStack

import concourse.mybir as mybir

K, T, S, H, N = 512, 2048, 1024, 512, 256
FLOPS = 2 * K * H * S + 2 * H * N * S

F32 = mybir.dt.float32
BF16 = mybir.dt.bfloat16
I32 = mybir.dt.int32
U32 = mybir.dt.uint32
U16 = mybir.dt.uint16
U8 = mybir.dt.uint8
FP8X4 = mybir.dt.float8_e4m3fn_x4
ADD = mybir.AluOpType.add

P = 128
PACK = 4
PER_COLUMN = 16
CHUNK = 128
HIDDEN_BANKS = 4
OUT_BANKS = 4
OUT_TILES = N // P
HALF = 64

FIRST_WORDS = 768
W1_PIECE = 128
GATHERS = ((0, 512), (512, 1024))
GPSIMD_ENTRIES = 96
POS_PIECES = ((0, 256), (256, 512)) + tuple((n0, n0 + CHUNK) for n0 in range(512, S, CHUNK))
W2_PIECE = 1
LAST_HALF = CHUNK // 2

W2_AT = 0
FIRST_PAIR_AT = 2048
ACROSS_BOTH_AT = 1536
ON_FIRST_PAIR_AT = 3072
PRODUCT_AT = 4096
PRODUCT_END_AT = 5120


def piece_of(pieces, n0):
    index = [i for i, (a, b) in enumerate(pieces) if a <= n0 < b][0]
    return index, n0 - pieces[index][0]


def tile_picked_embpos_none_p_kernel(tc, x_words, x_scales, w1, w2, pos, offs, out):
    nc = tc.nc
    with ExitStack() as ctx:
        keep = ctx.enter_context(tc.tile_pool(name="keep", bufs=1))
        behind_gpsimd = ctx.enter_context(tc.tile_pool(name="behind_gpsimd", bufs=1))
        hidden_banks = ctx.enter_context(tc.psum_pool(name="hidden_banks", bufs=1))
        out_banks = ctx.enter_context(tc.psum_pool(name="out_banks", bufs=OUT_BANKS))

        def sbuf(shape, dtype, name, takes_over=None):
            return keep.tile(shape, dtype, name=name, tag=takes_over or name, align_bytes=256)

        def placed(shape, dtype, name, offset):
            return behind_gpsimd.tile(shape, dtype, name=name, offset=offset, align_bytes=256)

        offsets = keep.tile([P, S // PER_COLUMN], U16, name="offsets", align_bytes=256)
        nc.sync.dma_start(offsets[:], offs)

        w1_raw = [sbuf([P, PACK, W1_PIECE], F32, f"w1_raw{i}") for i in range(H // W1_PIECE)]

        table_scales = sbuf([P, T], U8, "table_scales")
        nc.vector.memset(table_scales[:].bitcast(I32), 0)
        table_words = sbuf([P, T], I32, "table_words")
        word_rows = x_words[0].rearrange("p n t -> p (n t)").bitcast(I32)
        nc.sync.dma_start(out=table_words[:, :FIRST_WORDS], in_=word_rows[:, :FIRST_WORDS])
        for r in range(4):
            nc.sync.dma_start(
                out=table_scales[r:P:32, :].bitcast(I32),
                in_=x_scales[0][r:16:4, :].bitcast(I32),
            )
        nc.sync.dma_start(out=table_words[:, FIRST_WORDS:], in_=word_rows[:, FIRST_WORDS:])

        w1_rows = w1.rearrange("(p j) c -> p j c", j=PACK)
        for i, raw in enumerate(w1_raw):
            nc.sync.dma_start(out=raw[:], in_=w1_rows[:, :, i * W1_PIECE : (i + 1) * W1_PIECE])

        pos_rows = pos.rearrange("(p t) n -> p t n", t=PACK)
        pos_sb = []
        w2_raw = sbuf([P, PACK, N], F32, "w2_raw")
        for g, (n0, n1) in enumerate(POS_PIECES):
            if g == W2_PIECE:
                nc.sync.dma_start(out=w2_raw[:], in_=w2.rearrange("(p j) m -> p j m", j=PACK))
            piece = sbuf([P, PACK, n1 - n0], F32, f"pos{g}")
            nc.sync.dma_start(out=piece[:], in_=pos_rows[:, :, n0:n1])
            pos_sb.append(piece)

        def pos_at(n0, width):
            g, in_piece = piece_of(POS_PIECES, n0)
            return pos_sb[g][:, :, in_piece : in_piece + width]

        x_scale = sbuf([P, S], U8, "x_scale")
        nc.vector.tensor_copy(x_scale[:], table_scales[:].indirect(offsets[:]))
        x_codes = []

        def gather_words(g, takes_over=None):
            n0, n1 = GATHERS[g]
            x_codes.append(sbuf([P, n1 - n0], U32, f"x_codes{g}", takes_over))
            nc.vector.tensor_copy(
                x_codes[g][:],
                table_words[:].bitcast(U32).indirect(offsets[:, n0 // PER_COLUMN : n1 // PER_COLUMN]),
            )

        gather_words(0)

        w1_grouped = [sbuf([P, PACK, HALF, PACK], BF16, f"w1_grouped{half}") for half in range(2)]
        w1_codes = sbuf([P, H], U32, "w1_codes")
        w1_scale = sbuf([P, H], U8, "w1_scale")

        def lay_out_w1(copy, i, t0, t1):
            half, m0 = divmod(i * W1_PIECE // PACK, HALF)
            copy(
                out=w1_grouped[half][:, t0:t1, m0 : m0 + W1_PIECE // PACK, :].rearrange("p t m j -> p m j t"),
                in_=w1_raw[i][:].rearrange("p j (m t) -> p m j t", t=PACK)[:, :, :, t0:t1],
            )

        def quantise_w1(half):
            for t in range(PACK):
                cols = slice(t * P + half * HALF, t * P + (half + 1) * HALF)
                nc.vector.quantize_mx(
                    out=w1_codes[:, cols].bitcast(FP8X4),
                    scales=w1_scale[:, cols],
                    in_=w1_grouped[half][:, t, :, :].rearrange("p m j -> p (m j)"),
                )

        lay_out_w1(nc.scalar.copy, 0, 0, PACK)
        lay_out_w1(nc.scalar.copy, 1, 0, PACK)
        quantise_w1(0)
        lay_out_w1(nc.scalar.copy, 2, 0, PACK)
        lay_out_w1(nc.scalar.copy, 3, 0, 2)
        lay_out_w1(nc.vector.tensor_copy, 3, 2, PACK)
        quantise_w1(1)

        gather_words(1, "w1_raw3")

        w2_grouped = placed([P, N, PACK], BF16, "w2_grouped", W2_AT)
        w2_codes = sbuf([P, N], U32, "w2_codes")
        w2_scale = sbuf([P, N], U8, "w2_scale")
        for b in range(OUT_TILES):
            nc.scalar.copy(
                out=w2_grouped[:, b * P : (b + 1) * P, :].rearrange("p (c i) j -> p c j i", i=2),
                in_=w2_raw[:, :, b * P : (b + 1) * P].rearrange("p j (c i) -> p c j i", i=2),
            )

        first_banks = []

        def first_product(n0, width):
            gather, in_gather = piece_of(GATHERS, n0)
            bank = hidden_banks.tile(
                [P, PACK, width], F32, name="hidden_bank", tag=f"bank{len(first_banks) % HIDDEN_BANKS}"
            )
            first_banks.append(bank)
            for t in range(PACK):
                nc.tensor.matmul_mx(
                    out=bank[:, t, :],
                    lhsT=w1_codes[:, t * P : (t + 1) * P].bitcast(FP8X4),
                    lhsT_scale=w1_scale[:, t * P : (t + 1) * P],
                    rhs=x_codes[gather][:, in_gather : in_gather + width].bitcast(FP8X4),
                    rhs_scale=x_scale[:, n0 : n0 + width],
                    start=True,
                    stop=True,
                )
            return bank

        def add_pos(hidden, product, n0, width):
            nc.vector.tensor_tensor(
                out=hidden.rearrange("p (c i) t -> p c t i", i=2),
                in0=product.rearrange("p t (c i) -> p c t i", i=2),
                in1=pos_at(n0, width).rearrange("p t (c i) -> p c t i", i=2),
                op=ADD,
            )

        def first_layer(hidden, n0, width):
            add_pos(hidden, first_product(n0, width)[:], n0, width)

        def quantise(codes, scale, values):
            nc.vector.quantize_mx(out=codes.bitcast(FP8X4), scales=scale, in_=values.rearrange("p n t -> p (n t)"))

        def second_product(bank, b, codes, scale):
            nc.tensor.matmul_mx(
                out=bank,
                lhsT=w2_codes[:, b * P : (b + 1) * P].bitcast(FP8X4),
                lhsT_scale=w2_scale[:, b * P : (b + 1) * P],
                rhs=codes.bitcast(FP8X4),
                rhs_scale=scale,
                start=True,
                stop=True,
            )

        out_rows = out.rearrange("(b p) n -> p b n", p=P)

        def second_layer(result, codes, scale, width):
            for b in range(OUT_TILES):
                bank = out_banks.tile([P, width], F32, name="out_bank")
                second_product(bank[:], b, codes, scale)
                nc.scalar.copy(out=result[:, b, :], in_=bank[:])

        h_scale = sbuf([P, S], U8, "h_scale")

        def leave_pair(codes, n0):
            result = sbuf([P, OUT_TILES, 2 * CHUNK], F32, f"result_{n0}")
            second_layer(result[:], codes, h_scale[:, n0 : n0 + 2 * CHUNK], 2 * CHUNK)
            nc.sync.dma_start(out=out_rows[:, :, n0 : n0 + 2 * CHUNK], in_=result[:])

        def leave_chunk(codes, n0, width=CHUNK):
            bank = out_banks.tile([P, OUT_TILES, width], F32, name="out_bank")
            for b in range(OUT_TILES):
                second_product(bank[:, b, :], b, codes, h_scale[:, n0 : n0 + width])
            result = sbuf([P, OUT_TILES, width], F32, f"result_{n0}")
            nc.scalar.copy(out=result[:], in_=bank[:])
            nc.sync.dma_start(out=out_rows[:, :, n0 : n0 + width], in_=result[:])

        hidden_0 = placed([P, 2 * CHUNK, PACK], BF16, "hidden_0", FIRST_PAIR_AT)
        first_layer(hidden_0[:, :CHUNK, :], 0, CHUNK)
        first_layer(hidden_0[:, CHUNK:, :], 128, CHUNK)
        shared_bank = first_product(256, CHUNK)
        on_gpsimd = slice(CHUNK - GPSIMD_ENTRIES, CHUNK)
        on_vector = slice(0, CHUNK - GPSIMD_ENTRIES)
        gpsimd_product = placed([P, GPSIMD_ENTRIES, PACK], F32, "gpsimd_product", PRODUCT_AT)
        nc.scalar.copy(out=gpsimd_product[:], in_=shared_bank[:, :, on_gpsimd].rearrange("p t n -> p n t"))
        codes_0 = sbuf([P, 2 * CHUNK], U32, "codes_0")
        quantise(codes_0[:, :CHUNK], h_scale[:, 0:128], hidden_0[:, :CHUNK, :])
        quantise(w2_codes[:, :P], w2_scale[:, :P], w2_grouped[:, :P, :])
        quantise(codes_0[:, CHUNK:], h_scale[:, 128:256], hidden_0[:, CHUNK:, :])
        quantise(w2_codes[:, P:], w2_scale[:, P:], w2_grouped[:, P:, :])

        hidden_256 = placed([P, CHUNK, PACK], BF16, "hidden_256", ACROSS_BOTH_AT)
        nc.gpsimd.tensor_tensor(
            out=hidden_256[:, on_gpsimd, :],
            in0=gpsimd_product[:],
            in1=pos_at(256 + on_gpsimd.start, GPSIMD_ENTRIES).rearrange("p t n -> p n t"),
            op=ADD,
        )
        leave_chunk(codes_0[:], 0, 2 * CHUNK)

        hidden_384 = placed([P, CHUNK, PACK], BF16, "hidden_384", ON_FIRST_PAIR_AT)
        hidden_512 = sbuf([P, 2 * CHUNK, PACK], BF16, "hidden_512")
        first_layer(hidden_384[:], 384, CHUNK)
        add_pos(hidden_256[:, on_vector, :], shared_bank[:, :, on_vector], 256, CHUNK - GPSIMD_ENTRIES)
        first_layer(hidden_512[:, :CHUNK, :], 512, CHUNK)
        first_layer(hidden_512[:, CHUNK:, :], 640, CHUNK)

        codes_256 = placed([P, 2 * CHUNK], U32, "codes_256", PRODUCT_AT)
        codes_512 = placed([P, 2 * CHUNK], U32, "codes_512", PRODUCT_END_AT)
        quantise(codes_256[:, :CHUNK], h_scale[:, 256:384], hidden_256[:])
        leave_chunk(codes_256[:, :CHUNK], 256)
        quantise(codes_256[:, CHUNK:], h_scale[:, 384:512], hidden_384[:])
        leave_chunk(codes_256[:, CHUNK:], 384)
        quantise(codes_512[:], h_scale[:, 512:768], hidden_512[:])
        leave_pair(codes_512[:], 512)

        hidden_768 = placed([P, CHUNK, PACK], BF16, "hidden_768", ACROSS_BOTH_AT)
        first_layer(hidden_768[:], 768, CHUNK)
        hidden_896 = sbuf([P, LAST_HALF, PACK], BF16, "hidden_896", "hidden_512")
        first_layer(hidden_896[:], 896, LAST_HALF)
        codes_768 = sbuf([P, CHUNK], U32, "codes_768")
        quantise(codes_768[:], h_scale[:, 768:896], hidden_768[:])
        hidden_960 = sbuf([P, LAST_HALF, PACK], BF16, "hidden_960")
        first_layer(hidden_960[:], 960, LAST_HALF)
        codes_896 = sbuf([P, CHUNK], U32, "codes_896")
        quantise(codes_896[:, :LAST_HALF], h_scale[:, 896:960], hidden_896[:])
        quantise(codes_896[:, LAST_HALF:], h_scale[:, 960:1024], hidden_960[:])

        result_768 = sbuf([P, OUT_TILES, CHUNK], F32, "result_768")
        bank_768 = hidden_banks.tile([P, OUT_TILES, CHUNK], F32, name="bank_768", tag="bank1")
        for b in range(OUT_TILES):
            second_product(bank_768[:, b, :], b, codes_768[:], h_scale[:, 768:896])
        nc.scalar.copy(out=result_768[:], in_=bank_768[:])
        nc.sync.dma_start(out=out_rows[:, :, 768:896], in_=result_768[:])

        result_896 = sbuf([P, OUT_TILES, CHUNK], F32, "result_896")
        bank_896 = hidden_banks.tile([P, OUT_TILES, LAST_HALF], F32, name="bank_896", tag="bank2")
        for b in range(OUT_TILES):
            second_product(bank_896[:, b, :], b, codes_896[:, :LAST_HALF], h_scale[:, 896:960])
        nc.scalar.copy(out=result_896[:, :, :LAST_HALF], in_=bank_896[:])
        bank_960 = out_banks.tile([P, OUT_TILES, LAST_HALF], F32, name="out_bank")
        for b in range(OUT_TILES):
            second_product(bank_960[:, b, :], b, codes_896[:, LAST_HALF:], h_scale[:, 960:1024])
        nc.scalar.copy(out=result_896[:, :, LAST_HALF:], in_=bank_960[:])
        nc.sync.dma_start(out=out_rows[:, :, 896:1024], in_=result_896[:])
